import numpy as np
import ml_dtypes


def mxq(x, axis, fmt="e4m3"):
    dtype, down = {"e4m3": (ml_dtypes.float8_e4m3fn, 7), "e5m2": (ml_dtypes.float8_e5m2, 14)}[fmt]
    v = np.moveaxis(np.asarray(x, np.float32).astype(ml_dtypes.bfloat16).astype(np.float64), axis, -1)
    blocks = v.reshape(v.shape[:-1] + (-1, 32))
    amax = np.abs(blocks).max(-1, keepdims=True)
    byte = np.maximum(np.where(amax > 0, np.frexp(amax)[1] - 1 + 127, 0) - down, 1)
    scale = np.exp2(byte - 127.0)
    codes = (blocks / scale).astype(np.float32).astype(dtype).astype(np.float64)
    return np.moveaxis((codes * scale).reshape(v.shape), -1, axis)


WIDE = False


def mx_kscale(k):
    if not WIDE:
        return np.ones(k)
    levels = np.array([10, -10, 5, -5, 0])
    if k % 512:
        return np.exp2(np.random.permutation(np.resize(levels, k // 32))).repeat(32)
    a = np.empty((k // 512, 16))
    for p in range(k // 512):
        a[p, :8] = np.random.permutation(np.resize(levels, 8))
        for g in range(8):
            far = levels[np.abs(levels - a[p, g]) >= 10]
            a[p, g + 8] = far[np.random.randint(len(far))]
    return np.exp2(a.ravel()).repeat(32)


def f64(x):
    return np.asarray(x).astype(np.float64)


def striped(idx):
    return np.tile(idx.reshape(-1, 16).T, (8, 1)).astype(np.uint16)


def unstriped(offs):
    return offs[:16].T.reshape(-1).astype(np.int64)


def pack_weight(w):
    k, n = w.shape
    w = f64(np.asarray(w, np.float32).astype(ml_dtypes.bfloat16)).reshape(k // 32, 32, n)
    amax = np.abs(w).max(1)
    byte = np.clip(np.where(amax > 0, np.frexp(amax)[1] - 1 + 127 - 7, 1), 1, 254)
    scaled = (w * np.exp2(127.0 - byte)[:, None, :]).reshape(k, n).astype(np.float32)
    words = np.ascontiguousarray(scaled.reshape(k // 512, 128, 4, n).transpose(0, 1, 3, 2)).astype(ml_dtypes.float8_e4m3fn).view(np.uint8)
    return words, np.ascontiguousarray(byte.astype(np.uint8).reshape(k // 512, 16, n))


def unpack_weight(words, scales):
    g, p, n, _ = words.shape
    vals = np.ascontiguousarray(words).view(ml_dtypes.float8_e4m3fn).astype(np.float64) * np.repeat(np.exp2(scales.astype(np.float64) - 127.0), 8, axis=1)[..., None]
    return vals.transpose(0, 1, 3, 2).reshape(g * 512, n)


def relu2(v):
    return np.maximum(v, 0.0) ** 2


K, T, E, C, N = 1536, 1536, 4, 256, 128


def by_expert(wq, xq):
    return np.concatenate([wq[e].T @ xq[:, e * C:(e + 1) * C] for e in range(E)], axis=1)


def setup_inputs():
    n = np.random.standard_normal
    s = mx_kscale(K)[:, None]
    packed = [pack_weight(m) for m in n((E, K, N)) / np.sqrt(K) / s[None]]
    return {
        "xT": (n((K, T)) * s).astype(np.float32),
        "xr": n((N, T)).astype(np.float32),
        "w_words": np.stack([m[0] for m in packed]),
        "w_scales": np.stack([m[1] for m in packed]),
        "b": (0.3 * n((N, E))).astype(np.float32),
        "gate": np.tile(np.random.uniform(0.2, 1.0, E * C), (N, 1)).astype(np.float32),
        "offs": striped(np.random.permutation(T)[:E * C]),
    }


def reference(xT, xr, w_words, w_scales, b, gate, offs):
    idx = unstriped(offs)
    w = np.stack([unpack_weight(w_words[e], w_scales[e]) for e in range(E)])
    xq = mxq(f64(xT)[:, idx], 0, "e4m3")
    y = by_expert(w, xq)
    y = relu2(y + np.repeat(f64(b), C, axis=1))
    out = f64(xr).copy()
    out[:, idx] += f64(gate) * y
    return out

@@ -1,0 +1,164 @@
+from contextlib import ExitStack
+
+import concourse.mybir as mybir
+
+K, T, E, C, N = 1536, 1536, 4, 256, 128
+SLOTS = E * C
+P = 128
+PACK = 4
+PASSES = K // (P * PACK)
+OFFSETS_PER_COLUMN = 16
+
+FLOPS = 2 * K * N * SLOTS
+
+F32 = mybir.dt.float32
+BF16 = mybir.dt.bfloat16
+I32 = mybir.dt.int32
+U32 = mybir.dt.uint32
+U16 = mybir.dt.uint16
+U8 = mybir.dt.uint8
+FP8X4 = mybir.dt.float8_e4m3fn_x4
+Act = mybir.ActivationFunctionType
+Alu = mybir.AluOpType
+
+LOADS = ((1024, 512), (1024, 512), (768, 512, 256))
+
+CHUNKS = (
+    ((512, 320), (512, 336), (512, 256)),
+    ((512, 272), (512, 288), (512, 320)),
+    ((512, 272), (256, 96), (512, 240), (256, 192)),
+)
+
+LAST_GATHERS = (
+    ((0, 512), ((0, 256), (256, 256))),
+    ((512, 512), ((512, 512),)),
+)
+
+SCATTERS = ((0, 512), (512, 512))
+
+STORES = ((0, 640), (640, 640), (1280, 256))
+
+RUN = 4
+
+
+def tile_moe_res_lin_relu2_kernel(tc, xT, xr, w_words, w_scales, b, gate, offs, out):
+    nc = tc.nc
+    with ExitStack() as ctx:
+        keep = ctx.enter_context(tc.tile_pool(name="keep", bufs=1))
+        psum = ctx.enter_context(tc.psum_pool(name="psum", bufs=1))
+
+        offsets = keep.tile([P, SLOTS // OFFSETS_PER_COLUMN], U16, name="offsets")
+        w_codes = keep.tile([P, E * PASSES, N], U32, name="w_codes", align_bytes=64)
+        w_bytes = keep.tile([P, E * PASSES, N], U8, name="w_bytes", align_bytes=64)
+        bias = keep.tile([P, E], F32, name="bias")
+        gates = keep.tile([P, SLOTS], F32, name="gates")
+        resid = keep.tile([P, T], F32, name="resid")
+        window = keep.tile([P, T], F32, name="window")
+        total = keep.tile([P, T], F32, name="total")
+        token_codes = [keep.tile([P, T], U32, name=f"token_codes{a}", align_bytes=64) for a in range(PASSES)]
+        token_bytes = keep.tile([P, T], U8, name="token_bytes", align_bytes=64)
+        slot_codes = [keep.tile([P, SLOTS], U32, name=f"slot_codes{a}", align_bytes=64) for a in range(PASSES)]
+        slot_bytes = keep.tile([P, SLOTS], U8, name="slot_bytes", align_bytes=64)
+        relu = keep.tile([P, SLOTS], F32, name="relu")
+        square = keep.tile([P, SLOTS], F32, name="square")
+        zeros = keep.tile([P, 8], F32, name="zeros")
+        table_load = keep.tile([P, 8], F32, name="table_load")
+
+        nc.vector.memset(zeros[:], 0.0)
+        nc.scalar.activation(table_load[:], zeros[:], Act.Relu)
+        nc.gpsimd.memset(token_bytes[:], 0)
+        nc.vector.memset(w_bytes[:].rearrange("p g n -> p (g n)").bitcast(I32), 0)
+        nc.vector.memset(window[:], 0.0)
+
+        raws = {}
+        for a in range(PASSES):
+            rows = xT[a * P * PACK : (a + 1) * P * PACK, :].rearrange("(p r) t -> p r t", r=PACK)
+            t0 = 0
+            for width in LOADS[a]:
+                raw = keep.tile([P, PACK, width], F32, name=f"raw{a}_{t0}")
+                nc.sync.dma_start(out=raw[:], in_=rows[:, :, t0 : t0 + width])
+                if not raws:
+                    nc.sync.dma_start(offsets[:], offs)
+                raws[a, t0] = raw
+                t0 += width
+        for quadrant in range(4):
+            nc.sync.dma_start(
+                out=w_bytes[32 * quadrant : 32 * quadrant + 4, :, :].bitcast(I32),
+                in_=w_scales[:, :, 4 * quadrant : 4 * quadrant + 4, :].rearrange("e a q n -> q (e a) n").bitcast(I32),
+            )
+        for e in range(0, E, 2):
+            nc.sync.dma_start(
+                out=w_codes[:, e * PASSES : (e + 2) * PASSES, :].rearrange("p g n -> p (g n)").bitcast(I32),
+                in_=w_words[e : e + 2].rearrange("e a p n r -> p (e a) (n r)").bitcast(I32),
+            )
+            if e == 0:
+                nc.sync.dma_start(out=bias[:], in_=b)
+        nc.sync.dma_start(out=gates[:], in_=gate)
+        nc.sync.dma_start(out=resid[:], in_=xr)
+
+        def by_runs(raw, t0, t1):
+            return raw[:, :, t0:t1].rearrange("p r (c i) -> p c r i", i=RUN)
+
+        def interleaved(packed, t0, t1):
+            return packed[:, t0:t1, :].rearrange("p (c i) r -> p c r i", i=RUN)
+
+        def round_and_quantise(a, t0, width, by_vector):
+            load0 = max(start for pass_, start in raws if pass_ == a and start <= t0)
+            raw, c0 = raws[a, load0], t0 - load0
+            packed = keep.tile([P, width, PACK], BF16, name=f"packed{a}_{t0}", align_bytes=64)
+            nc.vector.tensor_copy(out=interleaved(packed, 0, by_vector), in_=by_runs(raw, c0, c0 + by_vector))
+            nc.scalar.activation(
+                interleaved(packed, by_vector, width), by_runs(raw, c0 + by_vector, c0 + width), Act.Copy
+            )
+            nc.vector.quantize_mx(
+                out=token_codes[a][:, t0 : t0 + width].bitcast(FP8X4),
+                scales=token_bytes[4 * a : P, t0 : t0 + width],
+                in_=packed[:].rearrange("p t r -> p (t r)"),
+            )
+
+        def offsets_of(j0, slots):
+            return offsets[:, j0 // OFFSETS_PER_COLUMN : (j0 + slots) // OFFSETS_PER_COLUMN]
+
+        def gather(of_slots, of_tokens, j0, slots):
+            nc.vector.tensor_copy(out=of_slots[:, j0 : j0 + slots], in_=of_tokens[:].indirect(offsets_of(j0, slots)))
+
+        def expert(e):
+            slots = slice(e * C, (e + 1) * C)
+            acc = psum.tile([P, C], F32, name=f"acc{e}")
+            for a in range(PASSES):
+                nc.tensor.matmul_mx(
+                    out=acc[:],
+                    lhsT=w_codes[:, e * PASSES + a, :].bitcast(FP8X4),
+                    lhsT_scale=w_bytes[:, e * PASSES + a, :],
+                    rhs=slot_codes[a][:, slots].bitcast(FP8X4),
+                    rhs_scale=slot_bytes[4 * a : P, slots],
+                    start=(a == 0),
+                    stop=(a == PASSES - 1),
+                )
+            nc.scalar.activation(relu[:, slots], acc[:], Act.Relu, bias=bias[:, e : e + 1])
+            nc.scalar.activation(square[:, slots], relu[:, slots], Act.Square)
+
+        for a in range(PASSES):
+            t0 = 0
+            for width, by_vector in CHUNKS[a]:
+                round_and_quantise(a, t0, width, by_vector)
+                t0 += width
+            if a < PASSES - 1:
+                gather(slot_codes[a], token_codes[a], 0, SLOTS)
+
+        for (j0, slots), byte_gathers in LAST_GATHERS:
+            gather(slot_codes[PASSES - 1], token_codes[PASSES - 1], j0, slots)
+            for byte_j0, byte_slots in byte_gathers:
+                gather(slot_bytes, token_bytes, byte_j0, byte_slots)
+            for e in range(j0 // C, (j0 + slots) // C):
+                expert(e)
+
+        for j0, slots in SCATTERS:
+            cols = slice(j0, j0 + slots)
+            nc.vector.tensor_tensor(
+                window[:].indirect(offsets_of(j0, slots)), square[:, cols], gates[:, cols], Alu.mult
+            )
+        for t0, width in STORES:
+            cols = slice(t0, t0 + width)
+            nc.vector.tensor_tensor(total[:, cols], window[:, cols], resid[:, cols], Alu.add)
+            nc.sync.dma_start(out=out[:, cols], in_=total[:, cols])

@@ -38,7 +38,7 @@ SCATTERS = ((0, 512), (512, 512))
 
 STORES = ((0, 640), (640, 640), (1280, 256))
 
-RUN = 4
+RUN = 2
 
 
 def tile_moe_res_lin_relu2_kernel(tc, xT, xr, w_words, w_scales, b, gate, offs, out):

@@ -21,13 +21,11 @@ FP8X4 = mybir.dt.float8_e4m3fn_x4
 Act = mybir.ActivationFunctionType
 Alu = mybir.AluOpType
 
-LOADS = ((1024, 512), (1024, 512), (768, 512, 256))
+LOADS = ((1536,), (1024, 512), (768, 512, 256))
 
-CHUNKS = (
-    ((512, 320), (512, 336), (512, 256)),
-    ((512, 272), (512, 288), (512, 320)),
-    ((512, 272), (256, 96), (512, 240), (256, 192)),
-)
+VECTOR_SHARE = ((9,), (6, 6), (4, 6, 8))
+
+CHUNK = 512
 
 LAST_GATHERS = (
     ((0, 512), ((0, 256), (256, 256))),
@@ -36,7 +34,7 @@ LAST_GATHERS = (
 
 SCATTERS = ((0, 512), (512, 512))
 
-STORES = ((0, 640), (640, 640), (1280, 256))
+STORES = ((0, 384), (384, 384), (768, 384), (1152, 384))
 
 RUN = 2
 
@@ -81,19 +79,22 @@ def tile_moe_res_lin_relu2_kernel(tc, xT, xr, w_words, w_scales, b, gate, offs, 
                     nc.sync.dma_start(offsets[:], offs)
                 raws[a, t0] = raw
                 t0 += width
-        for quadrant in range(4):
+        for q in range(4):
             nc.sync.dma_start(
-                out=w_bytes[32 * quadrant : 32 * quadrant + 4, :, :].bitcast(I32),
-                in_=w_scales[:, :, 4 * quadrant : 4 * quadrant + 4, :].rearrange("e a q n -> q (e a) n").bitcast(I32),
+                out=w_bytes[q:P:32, :, :].bitcast(I32),
+                in_=w_scales[:, :, q:16:4, :].rearrange("e a q n -> q (e a) n").bitcast(I32),
             )
-        for e in range(0, E, 2):
+
+        def load_weights(e):
             nc.sync.dma_start(
                 out=w_codes[:, e * PASSES : (e + 2) * PASSES, :].rearrange("p g n -> p (g n)").bitcast(I32),
                 in_=w_words[e : e + 2].rearrange("e a p n r -> p (e a) (n r)").bitcast(I32),
             )
-            if e == 0:
-                nc.sync.dma_start(out=bias[:], in_=b)
+
+        load_weights(0)
+        nc.sync.dma_start(out=bias[:], in_=b)
         nc.sync.dma_start(out=gates[:], in_=gate)
+        load_weights(2)
         nc.sync.dma_start(out=resid[:], in_=xr)
 
         def by_runs(raw, t0, t1):
@@ -139,10 +140,12 @@ def tile_moe_res_lin_relu2_kernel(tc, xT, xr, w_words, w_scales, b, gate, offs, 
             nc.scalar.activation(square[:, slots], relu[:, slots], Act.Square)
 
         for a in range(PASSES):
-            t0 = 0
-            for width, by_vector in CHUNKS[a]:
-                round_and_quantise(a, t0, width, by_vector)
-                t0 += width
+            load0 = 0
+            for load_width, share in zip(LOADS[a], VECTOR_SHARE[a]):
+                for t0 in range(load0, load0 + load_width, CHUNK):
+                    width = min(CHUNK, load0 + load_width - t0)
+                    round_and_quantise(a, t0, width, width * share // 16)
+                load0 += load_width
             if a < PASSES - 1:
                 gather(slot_codes[a], token_codes[a], 0, SLOTS)
 

@@ -28,13 +28,14 @@ VECTOR_SHARE = ((9,), (6, 6), (4, 6, 8))
 CHUNK = 512
 
 LAST_GATHERS = (
-    ((0, 512), ((0, 256), (256, 256))),
-    ((512, 512), ((512, 512),)),
+    ((0, 256), ((0, 256),)),
+    ((256, 256), ((256, 256),)),
+    ((512, 512), ((512, 256), (768, 256))),
 )
 
 SCATTERS = ((0, 512), (512, 512))
 
-STORES = ((0, 384), (384, 384), (768, 384), (1152, 384))
+STORES = ((0, 256), (256, 256), (512, 256), (768, 256), (1024, 256), (1280, 256))
 
 RUN = 2
 

@@ -60,11 +60,7 @@ def tile_moe_res_lin_relu2_kernel(tc, xT, xr, w_words, w_scales, b, gate, offs, 
         slot_bytes = keep.tile([P, SLOTS], U8, name="slot_bytes", align_bytes=64)
         relu = keep.tile([P, SLOTS], F32, name="relu")
         square = keep.tile([P, SLOTS], F32, name="square")
-        zeros = keep.tile([P, 8], F32, name="zeros")
-        table_load = keep.tile([P, 8], F32, name="table_load")
 
-        nc.vector.memset(zeros[:], 0.0)
-        nc.scalar.activation(table_load[:], zeros[:], Act.Relu)
         nc.gpsimd.memset(token_bytes[:], 0)
         nc.vector.memset(w_bytes[:].rearrange("p g n -> p (g n)").bitcast(I32), 0)
         nc.vector.memset(window[:], 0.0)

@@ -21,11 +21,15 @@ FP8X4 = mybir.dt.float8_e4m3fn_x4
 Act = mybir.ActivationFunctionType
 Alu = mybir.AluOpType
 
-LOADS = ((1536,), (1024, 512), (768, 512, 256))
+WHOLE_ROWS = (0, 3, 0)
 
-VECTOR_SHARE = ((9,), (6, 6), (4, 6, 8))
+LOADS = ((1536,), (768, 768), (768, 384, 256, 128))
 
-CHUNK = 512
+CHUNKS = (
+    ((512, 288), (512, 288), (512, 288)),
+    ((512, 224), (256, 128), (512, 256), (256, 128)),
+    ((256, None), (512, 64), (256, 64), (128, 0), (256, 64), (128, 64)),
+)
 
 LAST_GATHERS = (
     ((0, 256), ((0, 256),)),
@@ -68,13 +72,21 @@ def tile_moe_res_lin_relu2_kernel(tc, xT, xr, w_words, w_scales, b, gate, offs, 
         raws = {}
         for a in range(PASSES):
             rows = xT[a * P * PACK : (a + 1) * P * PACK, :].rearrange("(p r) t -> p r t", r=PACK)
+            first = WHOLE_ROWS[a]
+            if first:
+                raw = keep.tile([P, PACK, T], F32, name=f"raw{a}")
+                raws[a, 0] = raw
+                nc.sync.dma_start(out=raw[:, :first, :], in_=rows[:, :first, :])
             t0 = 0
             for width in LOADS[a]:
-                raw = keep.tile([P, PACK, width], F32, name=f"raw{a}_{t0}")
-                nc.sync.dma_start(out=raw[:], in_=rows[:, :, t0 : t0 + width])
-                if not raws:
+                if first:
+                    nc.sync.dma_start(out=raw[:, first:, t0 : t0 + width], in_=rows[:, first:, t0 : t0 + width])
+                else:
+                    raw = keep.tile([P, PACK, width], F32, name=f"raw{a}_{t0}")
+                    nc.sync.dma_start(out=raw[:], in_=rows[:, :, t0 : t0 + width])
+                    raws[a, t0] = raw
+                if a == 0 and t0 == 0:
                     nc.sync.dma_start(offsets[:], offs)
-                raws[a, t0] = raw
                 t0 += width
         for q in range(4):
             nc.sync.dma_start(
@@ -103,11 +115,16 @@ def tile_moe_res_lin_relu2_kernel(tc, xT, xr, w_words, w_scales, b, gate, offs, 
         def round_and_quantise(a, t0, width, by_vector):
             load0 = max(start for pass_, start in raws if pass_ == a and start <= t0)
             raw, c0 = raws[a, load0], t0 - load0
-            packed = keep.tile([P, width, PACK], BF16, name=f"packed{a}_{t0}", align_bytes=64)
-            nc.vector.tensor_copy(out=interleaved(packed, 0, by_vector), in_=by_runs(raw, c0, c0 + by_vector))
-            nc.scalar.activation(
-                interleaved(packed, by_vector, width), by_runs(raw, c0 + by_vector, c0 + width), Act.Copy
-            )
+            tag = "beside_gather" if (a, t0 + width) == (1, T) or by_vector is None else f"packed{a}_{t0}"
+            packed = keep.tile([P, width, PACK], BF16, name=f"packed{a}_{t0}", tag=tag, align_bytes=64)
+            if by_vector is None:
+                nc.gpsimd.tensor_copy(out=packed[:], in_=raw[:, :, c0 : c0 + width].rearrange("p r t -> p t r"))
+            if by_vector:
+                nc.vector.tensor_copy(out=interleaved(packed, 0, by_vector), in_=by_runs(raw, c0, c0 + by_vector))
+            if by_vector is not None and by_vector < width:
+                nc.scalar.activation(
+                    interleaved(packed, by_vector, width), by_runs(raw, c0 + by_vector, c0 + width), Act.Copy
+                )
             nc.vector.quantize_mx(
                 out=token_codes[a][:, t0 : t0 + width].bitcast(FP8X4),
                 scales=token_bytes[4 * a : P, t0 : t0 + width],
@@ -137,12 +154,10 @@ def tile_moe_res_lin_relu2_kernel(tc, xT, xr, w_words, w_scales, b, gate, offs, 
             nc.scalar.activation(square[:, slots], relu[:, slots], Act.Square)
 
         for a in range(PASSES):
-            load0 = 0
-            for load_width, share in zip(LOADS[a], VECTOR_SHARE[a]):
-                for t0 in range(load0, load0 + load_width, CHUNK):
-                    width = min(CHUNK, load0 + load_width - t0)
-                    round_and_quantise(a, t0, width, width * share // 16)
-                load0 += load_width
+            t0 = 0
+            for width, by_vector in CHUNKS[a]:
+                round_and_quantise(a, t0, width, by_vector)
+                t0 += width
             if a < PASSES - 1:
                 gather(slot_codes[a], token_codes[a], 0, SLOTS)
 

@@ -31,11 +31,7 @@ CHUNKS = (
     ((256, None), (512, 64), (256, 64), (128, 0), (256, 64), (128, 64)),
 )
 
-LAST_GATHERS = (
-    ((0, 256), ((0, 256),)),
-    ((256, 256), ((256, 256),)),
-    ((512, 512), ((512, 256), (768, 256))),
-)
+BYTE_GROUP = 2
 
 SCATTERS = ((0, 512), (512, 512))
 
@@ -161,12 +157,11 @@ def tile_moe_res_lin_relu2_kernel(tc, xT, xr, w_words, w_scales, b, gate, offs, 
             if a < PASSES - 1:
                 gather(slot_codes[a], token_codes[a], 0, SLOTS)
 
-        for (j0, slots), byte_gathers in LAST_GATHERS:
-            gather(slot_codes[PASSES - 1], token_codes[PASSES - 1], j0, slots)
-            for byte_j0, byte_slots in byte_gathers:
-                gather(slot_bytes, token_bytes, byte_j0, byte_slots)
-            for e in range(j0 // C, (j0 + slots) // C):
-                expert(e)
+        for e in range(E):
+            if e % BYTE_GROUP == 0:
+                gather(slot_bytes, token_bytes, e * C, BYTE_GROUP * C)
+            gather(slot_codes[PASSES - 1], token_codes[PASSES - 1], e * C, C)
+            expert(e)
 
         for j0, slots in SCATTERS:
             cols = slice(j0, j0 + slots)

@@ -7,6 +7,7 @@ SLOTS = E * C
 P = 128
 PACK = 4
 PASSES = K // (P * PACK)
+SCALE_ROWS = 4
 OFFSETS_PER_COLUMN = 16
 
 FLOPS = 2 * K * N * SLOTS
@@ -21,21 +22,18 @@ FP8X4 = mybir.dt.float8_e4m3fn_x4
 Act = mybir.ActivationFunctionType
 Alu = mybir.AluOpType
 
-WHOLE_ROWS = (0, 3, 0)
+LAST_LOADS = (768, 384, 256, 128)
 
-LOADS = ((1536,), (768, 768), (768, 384, 256, 128))
+CHUNKS = (512, 256, 128)
 
-CHUNKS = (
-    ((512, 288), (512, 288), (512, 288)),
-    ((512, 224), (256, 128), (512, 256), (256, 128)),
-    ((256, None), (512, 64), (256, 64), (128, 0), (256, 64), (128, 64)),
-)
+FIRST_PASS_SIXTEENTHS = 9
+LAST_PASS_BY_VECTOR = 48
 
-BYTE_GROUP = 2
+BY_GPSIMD = 256
 
-SCATTERS = ((0, 512), (512, 512))
+GROUP = 2
 
-STORES = ((0, 256), (256, 256), (512, 256), (768, 256), (1024, 256), (1280, 256))
+STORE = 256
 
 RUN = 2
 
@@ -65,65 +63,63 @@ def tile_moe_res_lin_relu2_kernel(tc, xT, xr, w_words, w_scales, b, gate, offs, 
         nc.vector.memset(w_bytes[:].rearrange("p g n -> p (g n)").bitcast(I32), 0)
         nc.vector.memset(window[:], 0.0)
 
-        raws = {}
-        for a in range(PASSES):
-            rows = xT[a * P * PACK : (a + 1) * P * PACK, :].rearrange("(p r) t -> p r t", r=PACK)
-            first = WHOLE_ROWS[a]
-            if first:
-                raw = keep.tile([P, PACK, T], F32, name=f"raw{a}")
-                raws[a, 0] = raw
-                nc.sync.dma_start(out=raw[:, :first, :], in_=rows[:, :first, :])
-            t0 = 0
-            for width in LOADS[a]:
-                if first:
-                    nc.sync.dma_start(out=raw[:, first:, t0 : t0 + width], in_=rows[:, first:, t0 : t0 + width])
-                else:
-                    raw = keep.tile([P, PACK, width], F32, name=f"raw{a}_{t0}")
-                    nc.sync.dma_start(out=raw[:], in_=rows[:, :, t0 : t0 + width])
-                    raws[a, t0] = raw
-                if a == 0 and t0 == 0:
-                    nc.sync.dma_start(offsets[:], offs)
-                t0 += width
-        for q in range(4):
+        rows = [
+            xT[a * P * PACK : (a + 1) * P * PACK, :].rearrange("(p r) t -> p r t", r=PACK) for a in range(PASSES)
+        ]
+        raw0 = keep.tile([P, PACK, T], F32, name="raw0")
+        nc.sync.dma_start(out=raw0[:], in_=rows[0])
+        nc.sync.dma_start(offsets[:], offs)
+        pieces = [[(0, T, raw0[:])], [], []]
+        raw1 = keep.tile([P, PACK, T], F32, name="raw1")
+        nc.sync.dma_start(out=raw1[:, : PACK - 1, :], in_=rows[1][:, : PACK - 1, :])
+        for t0 in (0, T // 2):
+            half = slice(t0, t0 + T // 2)
+            nc.sync.dma_start(out=raw1[:, PACK - 1 :, half], in_=rows[1][:, PACK - 1 :, half])
+            pieces[1].append((t0, T // 2, raw1[:, :, half]))
+        t0 = 0
+        for width in LAST_LOADS:
+            raw2 = keep.tile([P, PACK, width], F32, name=f"raw2_{t0}")
+            nc.sync.dma_start(out=raw2[:], in_=rows[2][:, :, t0 : t0 + width])
+            pieces[2].append((t0, width, raw2[:]))
+            t0 += width
+        for q in range(SCALE_ROWS):
             nc.sync.dma_start(
                 out=w_bytes[q:P:32, :, :].bitcast(I32),
-                in_=w_scales[:, :, q:16:4, :].rearrange("e a q n -> q (e a) n").bitcast(I32),
+                in_=w_scales[:, :, q:16:SCALE_ROWS, :].rearrange("e a q n -> q (e a) n").bitcast(I32),
             )
 
         def load_weights(e):
             nc.sync.dma_start(
-                out=w_codes[:, e * PASSES : (e + 2) * PASSES, :].rearrange("p g n -> p (g n)").bitcast(I32),
-                in_=w_words[e : e + 2].rearrange("e a p n r -> p (e a) (n r)").bitcast(I32),
+                out=w_codes[:, e * PASSES : (e + GROUP) * PASSES, :].rearrange("p g n -> p (g n)").bitcast(I32),
+                in_=w_words[e : e + GROUP].rearrange("e a p n r -> p (e a) (n r)").bitcast(I32),
             )
 
         load_weights(0)
         nc.sync.dma_start(out=bias[:], in_=b)
         nc.sync.dma_start(out=gates[:], in_=gate)
-        load_weights(2)
+        load_weights(GROUP)
         nc.sync.dma_start(out=resid[:], in_=xr)
 
-        def by_runs(raw, t0, t1):
-            return raw[:, :, t0:t1].rearrange("p r (c i) -> p c r i", i=RUN)
+        def by_runs(raw, i0, i1):
+            return raw[:, :, i0:i1].rearrange("p r (c i) -> p c r i", i=RUN)
 
-        def interleaved(packed, t0, t1):
-            return packed[:, t0:t1, :].rearrange("p (c i) r -> p c r i", i=RUN)
+        def interleaved(packed, i0, i1):
+            return packed[:, i0:i1, :].rearrange("p (c i) r -> p c r i", i=RUN)
 
-        def round_and_quantise(a, t0, width, by_vector):
-            load0 = max(start for pass_, start in raws if pass_ == a and start <= t0)
-            raw, c0 = raws[a, load0], t0 - load0
-            tag = "beside_gather" if (a, t0 + width) == (1, T) or by_vector is None else f"packed{a}_{t0}"
+        def round_and_quantise(a, t0, width, raw):
+            by_gpsimd = a == PASSES - 1 and t0 == 0
+            last_before_gather = a == PASSES - 2 and t0 + width == T
+            tag = "beside_gather" if by_gpsimd or last_before_gather else f"packed{a}_{t0}"
             packed = keep.tile([P, width, PACK], BF16, name=f"packed{a}_{t0}", tag=tag, align_bytes=64)
-            if by_vector is None:
-                nc.gpsimd.tensor_copy(out=packed[:], in_=raw[:, :, c0 : c0 + width].rearrange("p r t -> p t r"))
-            if by_vector:
-                nc.vector.tensor_copy(out=interleaved(packed, 0, by_vector), in_=by_runs(raw, c0, c0 + by_vector))
-            if by_vector is not None and by_vector < width:
-                nc.scalar.activation(
-                    interleaved(packed, by_vector, width), by_runs(raw, c0 + by_vector, c0 + width), Act.Copy
-                )
+            if by_gpsimd:
+                nc.gpsimd.tensor_copy(out=packed[:], in_=raw.rearrange("p r t -> p t r"))
+            else:
+                by_vector = (width * FIRST_PASS_SIXTEENTHS // 16, width // 2, LAST_PASS_BY_VECTOR)[a]
+                nc.vector.tensor_copy(out=interleaved(packed, 0, by_vector), in_=by_runs(raw, 0, by_vector))
+                nc.scalar.activation(interleaved(packed, by_vector, width), by_runs(raw, by_vector, width), Act.Copy)
             nc.vector.quantize_mx(
                 out=token_codes[a][:, t0 : t0 + width].bitcast(FP8X4),
-                scales=token_bytes[4 * a : P, t0 : t0 + width],
+                scales=token_bytes[SCALE_ROWS * a : P, t0 : t0 + width],
                 in_=packed[:].rearrange("p t r -> p (t r)"),
             )
 
@@ -134,41 +130,46 @@ def tile_moe_res_lin_relu2_kernel(tc, xT, xr, w_words, w_scales, b, gate, offs, 
             nc.vector.tensor_copy(out=of_slots[:, j0 : j0 + slots], in_=of_tokens[:].indirect(offsets_of(j0, slots)))
 
         def expert(e):
-            slots = slice(e * C, (e + 1) * C)
+            cols = slice(e * C, (e + 1) * C)
             acc = psum.tile([P, C], F32, name=f"acc{e}")
             for a in range(PASSES):
                 nc.tensor.matmul_mx(
                     out=acc[:],
                     lhsT=w_codes[:, e * PASSES + a, :].bitcast(FP8X4),
                     lhsT_scale=w_bytes[:, e * PASSES + a, :],
-                    rhs=slot_codes[a][:, slots].bitcast(FP8X4),
-                    rhs_scale=slot_bytes[4 * a : P, slots],
+                    rhs=slot_codes[a][:, cols].bitcast(FP8X4),
+                    rhs_scale=slot_bytes[SCALE_ROWS * a : P, cols],
                     start=(a == 0),
                     stop=(a == PASSES - 1),
                 )
-            nc.scalar.activation(relu[:, slots], acc[:], Act.Relu, bias=bias[:, e : e + 1])
-            nc.scalar.activation(square[:, slots], relu[:, slots], Act.Square)
+            nc.scalar.activation(relu[:, cols], acc[:], Act.Relu, bias=bias[:, e : e + 1])
+            nc.scalar.activation(square[:, cols], relu[:, cols], Act.Square)
 
         for a in range(PASSES):
-            t0 = 0
-            for width, by_vector in CHUNKS[a]:
-                round_and_quantise(a, t0, width, by_vector)
-                t0 += width
+            for t0, width, raw in pieces[a]:
+                i0 = 0
+                while i0 < width:
+                    if a == PASSES - 1 and t0 + i0 == 0:
+                        chunk = BY_GPSIMD
+                    else:
+                        chunk = max(c for c in CHUNKS if c <= width - i0)
+                    round_and_quantise(a, t0 + i0, chunk, raw[:, :, i0 : i0 + chunk])
+                    i0 += chunk
             if a < PASSES - 1:
                 gather(slot_codes[a], token_codes[a], 0, SLOTS)
 
         for e in range(E):
-            if e % BYTE_GROUP == 0:
-                gather(slot_bytes, token_bytes, e * C, BYTE_GROUP * C)
+            if e % GROUP == 0:
+                gather(slot_bytes, token_bytes, e * C, GROUP * C)
             gather(slot_codes[PASSES - 1], token_codes[PASSES - 1], e * C, C)
             expert(e)
 
-        for j0, slots in SCATTERS:
-            cols = slice(j0, j0 + slots)
+        for j0 in range(0, SLOTS, GROUP * C):
+            cols = slice(j0, j0 + GROUP * C)
             nc.vector.tensor_tensor(
-                window[:].indirect(offsets_of(j0, slots)), square[:, cols], gates[:, cols], Alu.mult
+                window[:].indirect(offsets_of(j0, GROUP * C)), square[:, cols], gates[:, cols], Alu.mult
             )
-        for t0, width in STORES:
-            cols = slice(t0, t0 + width)
+        for t0 in range(0, T, STORE):
+            cols = slice(t0, t0 + STORE)
             nc.vector.tensor_tensor(total[:, cols], window[:, cols], resid[:, cols], Alu.add)
             nc.sync.dma_start(out=out[:, cols], in_=total[:, cols])

@@ -27,13 +27,13 @@ LAST_LOADS = (768, 384, 256, 128)
 CHUNKS = (512, 256, 128)
 
 FIRST_PASS_SIXTEENTHS = 9
-LAST_PASS_BY_VECTOR = 48
+LAST_PASS_BY_VECTOR = 64
 
 BY_GPSIMD = 256
 
 GROUP = 2
 
-STORE = 256
+STORES = (192, 256, 320, 384, 384)
 
 RUN = 2
 
@@ -115,7 +115,10 @@ def tile_moe_res_lin_relu2_kernel(tc, xT, xr, w_words, w_scales, b, gate, offs, 
                 nc.gpsimd.tensor_copy(out=packed[:], in_=raw.rearrange("p r t -> p t r"))
             else:
                 by_vector = (width * FIRST_PASS_SIXTEENTHS // 16, width // 2, LAST_PASS_BY_VECTOR)[a]
-                nc.vector.tensor_copy(out=interleaved(packed, 0, by_vector), in_=by_runs(raw, 0, by_vector))
+                if a == PASSES - 1 and t0 < LAST_LOADS[0]:
+                    by_vector = 0
+                else:
+                    nc.vector.tensor_copy(out=interleaved(packed, 0, by_vector), in_=by_runs(raw, 0, by_vector))
                 nc.scalar.activation(interleaved(packed, by_vector, width), by_runs(raw, by_vector, width), Act.Copy)
             nc.vector.quantize_mx(
                 out=token_codes[a][:, t0 : t0 + width].bitcast(FP8X4),
@@ -169,7 +172,9 @@ def tile_moe_res_lin_relu2_kernel(tc, xT, xr, w_words, w_scales, b, gate, offs, 
             nc.vector.tensor_tensor(
                 window[:].indirect(offsets_of(j0, GROUP * C)), square[:, cols], gates[:, cols], Alu.mult
             )
-        for t0 in range(0, T, STORE):
-            cols = slice(t0, t0 + STORE)
+        t0 = 0
+        for width in STORES:
+            cols = slice(t0, t0 + width)
             nc.vector.tensor_tensor(total[:, cols], window[:, cols], resid[:, cols], Alu.add)
             nc.sync.dma_start(out=out[:, cols], in_=total[:, cols])
+            t0 += width

@@ -56,7 +56,6 @@ def tile_moe_res_lin_relu2_kernel(tc, xT, xr, w_words, w_scales, b, gate, offs, 
         token_bytes = keep.tile([P, T], U8, name="token_bytes", align_bytes=64)
         slot_codes = [keep.tile([P, SLOTS], U32, name=f"slot_codes{a}", align_bytes=64) for a in range(PASSES)]
         slot_bytes = keep.tile([P, SLOTS], U8, name="slot_bytes", align_bytes=64)
-        relu = keep.tile([P, SLOTS], F32, name="relu")
         square = keep.tile([P, SLOTS], F32, name="square")
 
         nc.gpsimd.memset(token_bytes[:], 0)
@@ -95,9 +94,10 @@ def tile_moe_res_lin_relu2_kernel(tc, xT, xr, w_words, w_scales, b, gate, offs, 
             )
 
         load_weights(0)
+        nc.sync.dma_start(out=gates[:, : GROUP * C], in_=gate[:, : GROUP * C])
         nc.sync.dma_start(out=bias[:], in_=b)
-        nc.sync.dma_start(out=gates[:], in_=gate)
         load_weights(GROUP)
+        nc.sync.dma_start(out=gates[:, GROUP * C :], in_=gate[:, GROUP * C :])
         nc.sync.dma_start(out=resid[:], in_=xr)
 
         def by_runs(raw, i0, i1):
@@ -132,9 +132,9 @@ def tile_moe_res_lin_relu2_kernel(tc, xT, xr, w_words, w_scales, b, gate, offs, 
         def gather(of_slots, of_tokens, j0, slots):
             nc.vector.tensor_copy(out=of_slots[:, j0 : j0 + slots], in_=of_tokens[:].indirect(offsets_of(j0, slots)))
 
-        def expert(e):
-            cols = slice(e * C, (e + 1) * C)
-            acc = psum.tile([P, C], F32, name=f"acc{e}")
+        def products(e, j0, slots):
+            cols = slice(j0, j0 + slots)
+            acc = psum.tile([P, slots], F32, name=f"acc{j0}")
             for a in range(PASSES):
                 nc.tensor.matmul_mx(
                     out=acc[:],
@@ -145,8 +145,7 @@ def tile_moe_res_lin_relu2_kernel(tc, xT, xr, w_words, w_scales, b, gate, offs, 
                     start=(a == 0),
                     stop=(a == PASSES - 1),
                 )
-            nc.scalar.activation(relu[:, cols], acc[:], Act.Relu, bias=bias[:, e : e + 1])
-            nc.scalar.activation(square[:, cols], relu[:, cols], Act.Square)
+            return acc
 
         for a in range(PASSES):
             for t0, width, raw in pieces[a]:
@@ -161,17 +160,44 @@ def tile_moe_res_lin_relu2_kernel(tc, xT, xr, w_words, w_scales, b, gate, offs, 
             if a < PASSES - 1:
                 gather(slot_codes[a], token_codes[a], 0, SLOTS)
 
+        accs = []
         for e in range(E):
-            if e % GROUP == 0:
-                gather(slot_bytes, token_bytes, e * C, GROUP * C)
-            gather(slot_codes[PASSES - 1], token_codes[PASSES - 1], e * C, C)
-            expert(e)
+            if e < 2:
+                gather(slot_bytes, token_bytes, e * C, C)
+            elif e == 2:
+                gather(slot_bytes, token_bytes, e * C, 2 * C)
+            if e < 2:
+                halves = []
+                for j0 in (e * C, e * C + C // 2):
+                    gather(slot_codes[PASSES - 1], token_codes[PASSES - 1], j0, C // 2)
+                    halves.append(products(e, j0, C // 2))
+                accs.append(halves)
+            else:
+                gather(slot_codes[PASSES - 1], token_codes[PASSES - 1], e * C, C)
+                accs.append(products(e, e * C, C))
 
-        for j0 in range(0, SLOTS, GROUP * C):
-            cols = slice(j0, j0 + GROUP * C)
-            nc.vector.tensor_tensor(
-                window[:].indirect(offsets_of(j0, GROUP * C)), square[:, cols], gates[:, cols], Alu.mult
-            )
+        gated0 = keep.tile([P, C], F32, name="gated0", tag="held")
+        relu0 = keep.tile([P, C], F32, name="relu0", tag="relu0")
+        for h in range(2):
+            cols = slice(h * C // 2, (h + 1) * C // 2)
+            nc.scalar.activation(relu0[:, cols], accs[0][h][:], Act.Relu, bias=bias[:, 0:1])
+            nc.scalar.activation(square[:, cols], relu0[:, cols], Act.Square)
+            nc.gpsimd.tensor_tensor(gated0[:, cols], square[:, cols], gates[:, cols], Alu.mult)
+        relu1 = keep.tile([P, C], F32, name="relu1", tag="relu0")
+        for h in range(2):
+            cols = slice(h * C // 2, (h + 1) * C // 2)
+            nc.scalar.activation(relu1[:, cols], accs[1][h][:], Act.Relu, bias=bias[:, 1:2])
+        gated1 = keep.tile([P, C], F32, name="gated1")
+        nc.gpsimd.tensor_tensor(gated1[:], relu1[:], gates[:, C : 2 * C], Alu.mult)
+        nc.scalar.activation(window[:].indirect(offsets_of(0, C)), gated0[:], Act.Copy)
+        nc.vector.tensor_tensor(window[:].indirect(offsets_of(C, C)), relu1[:], gated1[:], Alu.mult)
+        relu23 = keep.tile([P, 2, C], F32, name="relu23", tag="held")
+        for e in (2, 3):
+            nc.scalar.activation(relu23[:, e - 2, :], accs[e][:], Act.Relu, bias=bias[:, e : e + 1])
+            nc.scalar.activation(square[:, e * C : (e + 1) * C], relu23[:, e - 2, :], Act.Square)
+        nc.vector.tensor_tensor(
+            window[:].indirect(offsets_of(2 * C, 2 * C)), square[:, 2 * C :], gates[:, 2 * C :], Alu.mult
+        )
         t0 = 0
         for width in STORES:
             cols = slice(t0, t0 + width)

@@ -23,6 +23,7 @@ Act = mybir.ActivationFunctionType
 Alu = mybir.AluOpType
 
 LAST_LOADS = (768, 384, 256, 128)
+LOADS = ((3, (T,)), (3, (768, 768)), (0, LAST_LOADS))
 
 CHUNKS = (512, 256, 128)
 
@@ -65,39 +66,50 @@ def tile_moe_res_lin_relu2_kernel(tc, xT, xr, w_words, w_scales, b, gate, offs, 
         rows = [
             xT[a * P * PACK : (a + 1) * P * PACK, :].rearrange("(p r) t -> p r t", r=PACK) for a in range(PASSES)
         ]
-        raw0 = keep.tile([P, PACK, T], F32, name="raw0")
-        nc.sync.dma_start(out=raw0[:], in_=rows[0])
-        nc.sync.dma_start(offsets[:], offs)
-        pieces = [[(0, T, raw0[:])], [], []]
-        raw1 = keep.tile([P, PACK, T], F32, name="raw1")
-        nc.sync.dma_start(out=raw1[:, : PACK - 1, :], in_=rows[1][:, : PACK - 1, :])
-        for t0 in (0, T // 2):
-            half = slice(t0, t0 + T // 2)
-            nc.sync.dma_start(out=raw1[:, PACK - 1 :, half], in_=rows[1][:, PACK - 1 :, half])
-            pieces[1].append((t0, T // 2, raw1[:, :, half]))
-        t0 = 0
-        for width in LAST_LOADS:
-            raw2 = keep.tile([P, PACK, width], F32, name=f"raw2_{t0}")
-            nc.sync.dma_start(out=raw2[:], in_=rows[2][:, :, t0 : t0 + width])
-            pieces[2].append((t0, width, raw2[:]))
-            t0 += width
+        pieces = [[] for a in range(PASSES)]
+        for a in range(PASSES):
+            whole, widths = LOADS[a]
+            if whole == 0:
+                t0 = 0
+                for width in widths:
+                    raw = keep.tile([P, PACK, width], F32, name=f"raw{a}_{t0}")
+                    nc.sync.dma_start(out=raw[:], in_=rows[a][:, :, t0 : t0 + width])
+                    pieces[a].append((t0, width, raw[:]))
+                    t0 += width
+                continue
+            raw = keep.tile([P, PACK, T], F32, name=f"raw{a}")
+            run = whole * T + widths[0]
+            nc.sync.dma_start(
+                out=raw[:].rearrange("p r t -> p (r t)")[:, :run], in_=rows[a].rearrange("p r t -> p (r t)")[:, :run]
+            )
+            if a == 0:
+                nc.sync.dma_start(offsets[:], offs)
+            t0 = 0
+            for width in widths:
+                cols = slice(t0, t0 + width)
+                if t0 > 0:
+                    nc.sync.dma_start(out=raw[:, whole:, cols], in_=rows[a][:, whole:, cols])
+                pieces[a].append((t0, width, raw[:, :, cols]))
+                t0 += width
+
+        def load_weights(e, experts):
+            nc.sync.dma_start(
+                out=w_codes[:, e * PASSES : (e + experts) * PASSES, :].rearrange("p g n -> p (g n)").bitcast(I32),
+                in_=w_words[e : e + experts].rearrange("e a p n r -> p (e a) (n r)").bitcast(I32),
+            )
+
+        load_weights(0, 1)
         for q in range(SCALE_ROWS):
             nc.sync.dma_start(
                 out=w_bytes[q:P:32, :, :].bitcast(I32),
                 in_=w_scales[:, :, q:16:SCALE_ROWS, :].rearrange("e a q n -> q (e a) n").bitcast(I32),
             )
 
-        def load_weights(e):
-            nc.sync.dma_start(
-                out=w_codes[:, e * PASSES : (e + GROUP) * PASSES, :].rearrange("p g n -> p (g n)").bitcast(I32),
-                in_=w_words[e : e + GROUP].rearrange("e a p n r -> p (e a) (n r)").bitcast(I32),
-            )
-
-        load_weights(0)
-        nc.sync.dma_start(out=gates[:, : GROUP * C], in_=gate[:, : GROUP * C])
         nc.sync.dma_start(out=bias[:], in_=b)
-        load_weights(GROUP)
-        nc.sync.dma_start(out=gates[:, GROUP * C :], in_=gate[:, GROUP * C :])
+        load_weights(1, 1)
+        nc.sync.dma_start(out=gates[:, : 2 * C], in_=gate[:, : 2 * C])
+        load_weights(2, 2)
+        nc.sync.dma_start(out=gates[:, 2 * C :], in_=gate[:, 2 * C :])
         nc.sync.dma_start(out=resid[:], in_=xr)
 
         def by_runs(raw, i0, i1):
@@ -140,7 +152,7 @@ def tile_moe_res_lin_relu2_kernel(tc, xT, xr, w_words, w_scales, b, gate, offs, 
                     out=acc[:],
                     lhsT=w_codes[:, e * PASSES + a, :].bitcast(FP8X4),
                     lhsT_scale=w_bytes[:, e * PASSES + a, :],
-                    rhs=slot_codes[a][:, cols].bitcast(FP8X4),
+                    rhs=(late[0][:] if (a, e) == (1, E - 1) else slot_codes[a][:, cols]).bitcast(FP8X4),
                     rhs_scale=slot_bytes[SCALE_ROWS * a : P, cols],
                     start=(a == 0),
                     stop=(a == PASSES - 1),
@@ -158,9 +170,10 @@ def tile_moe_res_lin_relu2_kernel(tc, xT, xr, w_words, w_scales, b, gate, offs, 
                     round_and_quantise(a, t0 + i0, chunk, raw[:, :, i0 : i0 + chunk])
                     i0 += chunk
             if a < PASSES - 1:
-                gather(slot_codes[a], token_codes[a], 0, SLOTS)
+                gather(slot_codes[a], token_codes[a], 0, SLOTS if a == 0 else SLOTS - C)
 
         accs = []
+        late = []
         for e in range(E):
             if e < 2:
                 gather(slot_bytes, token_bytes, e * C, C)
@@ -173,6 +186,10 @@ def tile_moe_res_lin_relu2_kernel(tc, xT, xr, w_words, w_scales, b, gate, offs, 
                     halves.append(products(e, j0, C // 2))
                 accs.append(halves)
             else:
+                if e == E - 1:
+                    last_tag = f"packed{PASSES - 1}_{T - LAST_LOADS[-1]}"
+                    late.append(keep.tile([P, C], U32, name="late_codes", tag=last_tag, align_bytes=64))
+                    nc.vector.tensor_copy(out=late[0][:], in_=token_codes[1][:].indirect(offsets_of(e * C, C)))
                 gather(slot_codes[PASSES - 1], token_codes[PASSES - 1], e * C, C)
                 accs.append(products(e, e * C, C))
 

@@ -55,9 +55,8 @@ def tile_moe_res_lin_relu2_kernel(tc, xT, xr, w_words, w_scales, b, gate, offs, 
         total = keep.tile([P, T], F32, name="total")
         token_codes = [keep.tile([P, T], U32, name=f"token_codes{a}", align_bytes=64) for a in range(PASSES)]
         token_bytes = keep.tile([P, T], U8, name="token_bytes", align_bytes=64)
-        slot_codes = [keep.tile([P, SLOTS], U32, name=f"slot_codes{a}", align_bytes=64) for a in range(PASSES)]
-        slot_bytes = keep.tile([P, SLOTS], U8, name="slot_bytes", align_bytes=64)
-        square = keep.tile([P, SLOTS], F32, name="square")
+        slot_codes = [keep.tile([P, SLOTS - C], U32, name=f"slot_codes{a}", align_bytes=64) for a in range(PASSES - 1)]
+        square = keep.tile([P, C], F32, name="square")
 
         nc.gpsimd.memset(token_bytes[:], 0)
         nc.vector.memset(w_bytes[:].rearrange("p g n -> p (g n)").bitcast(I32), 0)
@@ -144,21 +143,6 @@ def tile_moe_res_lin_relu2_kernel(tc, xT, xr, w_words, w_scales, b, gate, offs, 
         def gather(of_slots, of_tokens, j0, slots):
             nc.vector.tensor_copy(out=of_slots[:, j0 : j0 + slots], in_=of_tokens[:].indirect(offsets_of(j0, slots)))
 
-        def products(e, j0, slots):
-            cols = slice(j0, j0 + slots)
-            acc = psum.tile([P, slots], F32, name=f"acc{j0}")
-            for a in range(PASSES):
-                nc.tensor.matmul_mx(
-                    out=acc[:],
-                    lhsT=w_codes[:, e * PASSES + a, :].bitcast(FP8X4),
-                    lhsT_scale=w_bytes[:, e * PASSES + a, :],
-                    rhs=(late[0][:] if (a, e) == (1, E - 1) else slot_codes[a][:, cols]).bitcast(FP8X4),
-                    rhs_scale=slot_bytes[SCALE_ROWS * a : P, cols],
-                    start=(a == 0),
-                    stop=(a == PASSES - 1),
-                )
-            return acc
-
         for a in range(PASSES):
             for t0, width, raw in pieces[a]:
                 i0 = 0
@@ -170,51 +154,76 @@ def tile_moe_res_lin_relu2_kernel(tc, xT, xr, w_words, w_scales, b, gate, offs, 
                     round_and_quantise(a, t0 + i0, chunk, raw[:, :, i0 : i0 + chunk])
                     i0 += chunk
             if a < PASSES - 1:
-                gather(slot_codes[a], token_codes[a], 0, SLOTS if a == 0 else SLOTS - C)
+                gather(slot_codes[a], token_codes[a], 0, SLOTS - C)
 
+        def gather_tile(name, tag, dtype, of_tokens, j0, slots):
+            tile = keep.tile([P, slots], dtype, name=name, tag=tag, align_bytes=64)
+            nc.vector.tensor_copy(out=tile[:], in_=of_tokens[:].indirect(offsets_of(j0, slots)))
+            return tile
+
+        def multiply(name, e, words, scales):
+            acc = psum.tile([P, words[0].shape[1]], F32, name=name)
+            for a in range(PASSES):
+                nc.tensor.matmul_mx(
+                    out=acc[:],
+                    lhsT=w_codes[:, e * PASSES + a, :].bitcast(FP8X4),
+                    lhsT_scale=w_bytes[:, e * PASSES + a, :],
+                    rhs=words[a].bitcast(FP8X4),
+                    rhs_scale=scales[SCALE_ROWS * a : P, :],
+                    start=(a == 0),
+                    stop=(a == PASSES - 1),
+                )
+            return acc
+
+        def early_words(j0, slots):
+            return [slot_codes[a][:, j0 : j0 + slots] for a in range(PASSES - 1)]
+
+        def gpsimd_product(j0, relu):
+            cols = slice(j0, j0 + relu.shape[1])
+            once = keep.tile([P, relu.shape[1]], F32, name=f"once{j0}")
+            nc.gpsimd.tensor_tensor(once[:], relu, gates[:, cols], Alu.mult)
+            nc.gpsimd.tensor_tensor(gated[:, cols], once[:], relu, Alu.mult)
+
+        H = C // 2
+        last = token_codes[PASSES - 1]
+        gated = keep.tile([P, 2 * C], F32, name="gated")
         accs = []
-        late = []
-        for e in range(E):
-            if e < 2:
-                gather(slot_bytes, token_bytes, e * C, C)
-            elif e == 2:
-                gather(slot_bytes, token_bytes, e * C, 2 * C)
-            if e < 2:
-                halves = []
-                for j0 in (e * C, e * C + C // 2):
-                    gather(slot_codes[PASSES - 1], token_codes[PASSES - 1], j0, C // 2)
-                    halves.append(products(e, j0, C // 2))
-                accs.append(halves)
-            else:
-                if e == E - 1:
-                    last_tag = f"packed{PASSES - 1}_{T - LAST_LOADS[-1]}"
-                    late.append(keep.tile([P, C], U32, name="late_codes", tag=last_tag, align_bytes=64))
-                    nc.vector.tensor_copy(out=late[0][:], in_=token_codes[1][:].indirect(offsets_of(e * C, C)))
-                gather(slot_codes[PASSES - 1], token_codes[PASSES - 1], e * C, C)
-                accs.append(products(e, e * C, C))
+        for e in range(2):
+            scales = gather_tile(f"bytes{e}", f"bytes{e}", U8, token_bytes, e * C, C)
+            for h in range(2):
+                j0 = e * C + h * H
+                words = gather_tile(f"words{j0}", f"words{j0}", U32, last, j0, H)
+                accs.append(multiply(f"acc{j0}", e, early_words(j0, H) + [words[:]], scales[:, h * H : (h + 1) * H]))
+        bytes23 = gather_tile("bytes23", "bytes23", U8, token_bytes, 2 * C, 2 * C)
+        words2 = gather_tile("words2", "words2", U32, last, 2 * C, C)
+        acc2 = multiply("acc2", 2, early_words(2 * C, C) + [words2[:]], bytes23[:, :C])
+        last_tag = f"packed{PASSES - 1}_{T - LAST_LOADS[-1]}"
+        words3 = keep.tile([P, PASSES, C], U32, name="words3", tag=last_tag, align_bytes=64)
+        for a in range(PASSES):
+            nc.vector.tensor_copy(out=words3[:, a, :], in_=token_codes[a][:].indirect(offsets_of(3 * C, C)))
+        acc3 = multiply("acc3", 3, [words3[:, a, :] for a in range(PASSES)], bytes23[:, C:])
 
-        gated0 = keep.tile([P, C], F32, name="gated0", tag="held")
         relu0 = keep.tile([P, C], F32, name="relu0", tag="relu0")
         for h in range(2):
-            cols = slice(h * C // 2, (h + 1) * C // 2)
-            nc.scalar.activation(relu0[:, cols], accs[0][h][:], Act.Relu, bias=bias[:, 0:1])
+            cols = slice(h * H, (h + 1) * H)
+            nc.scalar.activation(relu0[:, cols], accs[h][:], Act.Relu, bias=bias[:, 0:1])
             nc.scalar.activation(square[:, cols], relu0[:, cols], Act.Square)
-            nc.gpsimd.tensor_tensor(gated0[:, cols], square[:, cols], gates[:, cols], Alu.mult)
+            nc.gpsimd.tensor_tensor(gated[:, cols], square[:, cols], gates[:, cols], Alu.mult)
         relu1 = keep.tile([P, C], F32, name="relu1", tag="relu0")
         for h in range(2):
-            cols = slice(h * C // 2, (h + 1) * C // 2)
-            nc.scalar.activation(relu1[:, cols], accs[1][h][:], Act.Relu, bias=bias[:, 1:2])
-        gated1 = keep.tile([P, C], F32, name="gated1")
-        nc.gpsimd.tensor_tensor(gated1[:], relu1[:], gates[:, C : 2 * C], Alu.mult)
-        nc.scalar.activation(window[:].indirect(offsets_of(0, C)), gated0[:], Act.Copy)
-        nc.vector.tensor_tensor(window[:].indirect(offsets_of(C, C)), relu1[:], gated1[:], Alu.mult)
-        relu23 = keep.tile([P, 2, C], F32, name="relu23", tag="held")
-        for e in (2, 3):
-            nc.scalar.activation(relu23[:, e - 2, :], accs[e][:], Act.Relu, bias=bias[:, e : e + 1])
-            nc.scalar.activation(square[:, e * C : (e + 1) * C], relu23[:, e - 2, :], Act.Square)
-        nc.vector.tensor_tensor(
-            window[:].indirect(offsets_of(2 * C, 2 * C)), square[:, 2 * C :], gates[:, 2 * C :], Alu.mult
-        )
+            cols = slice(h * H, (h + 1) * H)
+            nc.scalar.activation(relu1[:, cols], accs[2 + h][:], Act.Relu, bias=bias[:, 1:2])
+        gpsimd_product(C, relu1[:])
+        relu23 = keep.tile([P, 2 * C], F32, name="relu23")
+        once23 = keep.tile([P, 2 * C], F32, name="once23")
+        nc.vector.tensor_scalar(relu23[:, :C], acc2[:], bias[:, 2:3], 0.0, Alu.add, Alu.max)
+        nc.gpsimd.tensor_tensor(once23[:, :C], relu23[:, :C], gates[:, 2 * C : 3 * C], Alu.mult)
+        nc.vector.tensor_scalar(relu23[:, C:], acc3[:], bias[:, 3:4], 0.0, Alu.add, Alu.max)
+        nc.vector.scalar_tensor_tensor(once23[:, C:], acc3[:], bias[:, 3:4], gates[:, 3 * C :], Alu.add, Alu.mult)
+
+        for e in range(2):
+            nc.scalar.activation(window[:].indirect(offsets_of(e * C, C)), gated[:, e * C : (e + 1) * C], Act.Copy)
+        nc.vector.tensor_tensor(window[:].indirect(offsets_of(2 * C, 2 * C)), relu23[:], once23[:], Alu.mult)
         t0 = 0
         for width in STORES:
             cols = slice(t0, t0 + width)

@@ -22,17 +22,19 @@ FP8X4 = mybir.dt.float8_e4m3fn_x4
 Act = mybir.ActivationFunctionType
 Alu = mybir.AluOpType
 
-LAST_LOADS = (768, 384, 256, 128)
+LAST_LOADS = (640, 512, 256, 128)
 LOADS = ((3, (T,)), (3, (768, 768)), (0, LAST_LOADS))
 
 CHUNKS = (512, 256, 128)
+LAST_CHUNKS = (384, 256, 128)
+PLANES = (8, 4, 0)
 
 FIRST_PASS_SIXTEENTHS = 9
 LAST_PASS_BY_VECTOR = 64
 
 BY_GPSIMD = 256
 
-GROUP = 2
+EARLY_SLOTS = (3 * C + C // 2, 3 * C)
 
 STORES = (192, 256, 320, 384, 384)
 
@@ -55,7 +57,7 @@ def tile_moe_res_lin_relu2_kernel(tc, xT, xr, w_words, w_scales, b, gate, offs, 
         total = keep.tile([P, T], F32, name="total")
         token_codes = [keep.tile([P, T], U32, name=f"token_codes{a}", align_bytes=64) for a in range(PASSES)]
         token_bytes = keep.tile([P, T], U8, name="token_bytes", align_bytes=64)
-        slot_codes = [keep.tile([P, SLOTS - C], U32, name=f"slot_codes{a}", align_bytes=64) for a in range(PASSES - 1)]
+        slot_codes = [keep.tile([P, EARLY_SLOTS[a]], U32, name=f"slot_codes{a}", align_bytes=64) for a in range(PASSES - 1)]
         square = keep.tile([P, C], F32, name="square")
 
         nc.gpsimd.memset(token_bytes[:], 0)
@@ -125,7 +127,7 @@ def tile_moe_res_lin_relu2_kernel(tc, xT, xr, w_words, w_scales, b, gate, offs, 
             if by_gpsimd:
                 nc.gpsimd.tensor_copy(out=packed[:], in_=raw.rearrange("p r t -> p t r"))
             else:
-                by_vector = (width * FIRST_PASS_SIXTEENTHS // 16, width // 2, LAST_PASS_BY_VECTOR)[a]
+                by_vector = (width * FIRST_PASS_SIXTEENTHS // 16, width * 9 // 16, width * 6 // 16)[a]
                 if a == PASSES - 1 and t0 < LAST_LOADS[0]:
                     by_vector = 0
                 else:
@@ -133,7 +135,7 @@ def tile_moe_res_lin_relu2_kernel(tc, xT, xr, w_words, w_scales, b, gate, offs, 
                 nc.scalar.activation(interleaved(packed, by_vector, width), by_runs(raw, by_vector, width), Act.Copy)
             nc.vector.quantize_mx(
                 out=token_codes[a][:, t0 : t0 + width].bitcast(FP8X4),
-                scales=token_bytes[SCALE_ROWS * a : P, t0 : t0 + width],
+                scales=token_bytes[PLANES[a] : P, t0 : t0 + width],
                 in_=packed[:].rearrange("p t r -> p (t r)"),
             )
 
@@ -150,29 +152,32 @@ def tile_moe_res_lin_relu2_kernel(tc, xT, xr, w_words, w_scales, b, gate, offs, 
                     if a == PASSES - 1 and t0 + i0 == 0:
                         chunk = BY_GPSIMD
                     else:
-                        chunk = max(c for c in CHUNKS if c <= width - i0)
+                        chunk = max(c for c in (LAST_CHUNKS if a == PASSES - 1 else CHUNKS) if c <= width - i0 and width - i0 - c != P)
                     round_and_quantise(a, t0 + i0, chunk, raw[:, :, i0 : i0 + chunk])
                     i0 += chunk
             if a < PASSES - 1:
-                gather(slot_codes[a], token_codes[a], 0, SLOTS - C)
+                gather(slot_codes[a], token_codes[a], 0, EARLY_SLOTS[a])
 
         def gather_tile(name, tag, dtype, of_tokens, j0, slots):
             tile = keep.tile([P, slots], dtype, name=name, tag=tag, align_bytes=64)
             nc.vector.tensor_copy(out=tile[:], in_=of_tokens[:].indirect(offsets_of(j0, slots)))
             return tile
 
+        def one_pass(acc, e, a, words, scales, start=True):
+            nc.tensor.matmul_mx(
+                out=acc,
+                lhsT=w_codes[:, e * PASSES + a, :].bitcast(FP8X4),
+                lhsT_scale=w_bytes[:, e * PASSES + a, :],
+                rhs=words.bitcast(FP8X4),
+                rhs_scale=scales[PLANES[a] : P, :],
+                start=start and a == 0,
+                stop=(a == PASSES - 1),
+            )
+
         def multiply(name, e, words, scales):
             acc = psum.tile([P, words[0].shape[1]], F32, name=name)
             for a in range(PASSES):
-                nc.tensor.matmul_mx(
-                    out=acc[:],
-                    lhsT=w_codes[:, e * PASSES + a, :].bitcast(FP8X4),
-                    lhsT_scale=w_bytes[:, e * PASSES + a, :],
-                    rhs=words[a].bitcast(FP8X4),
-                    rhs_scale=scales[SCALE_ROWS * a : P, :],
-                    start=(a == 0),
-                    stop=(a == PASSES - 1),
-                )
+                one_pass(acc[:], e, a, words[a], scales)
             return acc
 
         def early_words(j0, slots):
@@ -195,13 +200,21 @@ def tile_moe_res_lin_relu2_kernel(tc, xT, xr, w_words, w_scales, b, gate, offs, 
                 words = gather_tile(f"words{j0}", f"words{j0}", U32, last, j0, H)
                 accs.append(multiply(f"acc{j0}", e, early_words(j0, H) + [words[:]], scales[:, h * H : (h + 1) * H]))
         bytes23 = gather_tile("bytes23", "bytes23", U8, token_bytes, 2 * C, 2 * C)
-        words2 = gather_tile("words2", "words2", U32, last, 2 * C, C)
-        acc2 = multiply("acc2", 2, early_words(2 * C, C) + [words2[:]], bytes23[:, :C])
         last_tag = f"packed{PASSES - 1}_{T - LAST_LOADS[-1]}"
-        words3 = keep.tile([P, PASSES, C], U32, name="words3", tag=last_tag, align_bytes=64)
-        for a in range(PASSES):
-            nc.vector.tensor_copy(out=words3[:, a, :], in_=token_codes[a][:].indirect(offsets_of(3 * C, C)))
-        acc3 = multiply("acc3", 3, [words3[:, a, :] for a in range(PASSES)], bytes23[:, C:])
+        late = keep.tile([P, H + C], U32, name="late", tag=last_tag, align_bytes=64)
+        nc.vector.tensor_copy(out=late[:, :H], in_=token_codes[0][:].indirect(offsets_of(3 * C + H, H)))
+        nc.vector.tensor_copy(out=late[:, H:], in_=token_codes[1][:].indirect(offsets_of(3 * C, C)))
+        words2 = gather_tile("words2", "words2", U32, last, 2 * C, C)
+        words3 = gather_tile("words3", "words3", U32, last, 3 * C, C)
+        acc2 = psum.tile([P, C], F32, name="acc2")
+        acc3 = psum.tile([P, C], F32, name="acc3")
+        one_pass(acc2[:], 2, 0, slot_codes[0][:, 2 * C : 3 * C], bytes23[:, :C])
+        one_pass(acc3[:, :H], 3, 0, slot_codes[0][:, 3 * C :], bytes23[:, C : C + H])
+        one_pass(acc2[:], 2, 1, slot_codes[1][:, 2 * C :], bytes23[:, :C])
+        one_pass(acc3[:, H:], 3, 0, late[:, :H], bytes23[:, C + H :], start=False)
+        one_pass(acc3[:], 3, 1, late[:, H:], bytes23[:, C:])
+        one_pass(acc2[:], 2, 2, words2[:], bytes23[:, :C])
+        one_pass(acc3[:], 3, 2, words3[:], bytes23[:, C:])
 
         relu0 = keep.tile([P, C], F32, name="relu0", tag="relu0")
         for h in range(2):
@@ -217,7 +230,7 @@ def tile_moe_res_lin_relu2_kernel(tc, xT, xr, w_words, w_scales, b, gate, offs, 
         relu23 = keep.tile([P, 2 * C], F32, name="relu23")
         once23 = keep.tile([P, 2 * C], F32, name="once23")
         nc.vector.tensor_scalar(relu23[:, :C], acc2[:], bias[:, 2:3], 0.0, Alu.add, Alu.max)
-        nc.gpsimd.tensor_tensor(once23[:, :C], relu23[:, :C], gates[:, 2 * C : 3 * C], Alu.mult)
+        nc.vector.scalar_tensor_tensor(once23[:, :C], acc2[:], bias[:, 2:3], gates[:, 2 * C : 3 * C], Alu.add, Alu.mult)
         nc.vector.tensor_scalar(relu23[:, C:], acc3[:], bias[:, 3:4], 0.0, Alu.add, Alu.max)
         nc.vector.scalar_tensor_tensor(once23[:, C:], acc3[:], bias[:, 3:4], gates[:, 3 * C :], Alu.add, Alu.mult)
 

@@ -34,9 +34,9 @@ LAST_PASS_BY_VECTOR = 64
 
 BY_GPSIMD = 256
 
-EARLY_SLOTS = (3 * C + C // 2, 3 * C)
+EARLY_SLOTS = (SLOTS, 3 * C)
 
-STORES = (192, 256, 320, 384, 384)
+STORES = (256, 320, 320, 320, 320)
 
 RUN = 2
 
@@ -45,6 +45,7 @@ def tile_moe_res_lin_relu2_kernel(tc, xT, xr, w_words, w_scales, b, gate, offs, 
     nc = tc.nc
     with ExitStack() as ctx:
         keep = ctx.enter_context(tc.tile_pool(name="keep", bufs=1))
+        turns = ctx.enter_context(tc.tile_pool(name="turns", bufs=1))
         psum = ctx.enter_context(tc.psum_pool(name="psum", bufs=1))
 
         offsets = keep.tile([P, SLOTS // OFFSETS_PER_COLUMN], U16, name="offsets")
@@ -108,9 +109,9 @@ def tile_moe_res_lin_relu2_kernel(tc, xT, xr, w_words, w_scales, b, gate, offs, 
 
         nc.sync.dma_start(out=bias[:], in_=b)
         load_weights(1, 1)
-        nc.sync.dma_start(out=gates[:, : 2 * C], in_=gate[:, : 2 * C])
+        nc.sync.dma_start(out=gates[:, :C], in_=gate[:, :C])
+        nc.sync.dma_start(out=gates[:, C:], in_=gate[:, C:])
         load_weights(2, 2)
-        nc.sync.dma_start(out=gates[:, 2 * C :], in_=gate[:, 2 * C :])
         nc.sync.dma_start(out=resid[:], in_=xr)
 
         def by_runs(raw, i0, i1):
@@ -127,7 +128,7 @@ def tile_moe_res_lin_relu2_kernel(tc, xT, xr, w_words, w_scales, b, gate, offs, 
             if by_gpsimd:
                 nc.gpsimd.tensor_copy(out=packed[:], in_=raw.rearrange("p r t -> p t r"))
             else:
-                by_vector = (width * FIRST_PASS_SIXTEENTHS // 16, width * 9 // 16, width * 6 // 16)[a]
+                by_vector = (width * FIRST_PASS_SIXTEENTHS // 16, width * 8 // 16, width * 6 // 16)[a]
                 if a == PASSES - 1 and t0 < LAST_LOADS[0]:
                     by_vector = 0
                 else:
@@ -183,12 +184,6 @@ def tile_moe_res_lin_relu2_kernel(tc, xT, xr, w_words, w_scales, b, gate, offs, 
         def early_words(j0, slots):
             return [slot_codes[a][:, j0 : j0 + slots] for a in range(PASSES - 1)]
 
-        def gpsimd_product(j0, relu):
-            cols = slice(j0, j0 + relu.shape[1])
-            once = keep.tile([P, relu.shape[1]], F32, name=f"once{j0}")
-            nc.gpsimd.tensor_tensor(once[:], relu, gates[:, cols], Alu.mult)
-            nc.gpsimd.tensor_tensor(gated[:, cols], once[:], relu, Alu.mult)
-
         H = C // 2
         last = token_codes[PASSES - 1]
         gated = keep.tile([P, 2 * C], F32, name="gated")
@@ -199,34 +194,38 @@ def tile_moe_res_lin_relu2_kernel(tc, xT, xr, w_words, w_scales, b, gate, offs, 
                 j0 = e * C + h * H
                 words = gather_tile(f"words{j0}", f"words{j0}", U32, last, j0, H)
                 accs.append(multiply(f"acc{j0}", e, early_words(j0, H) + [words[:]], scales[:, h * H : (h + 1) * H]))
-        bytes23 = gather_tile("bytes23", "bytes23", U8, token_bytes, 2 * C, 2 * C)
-        last_tag = f"packed{PASSES - 1}_{T - LAST_LOADS[-1]}"
-        late = keep.tile([P, H + C], U32, name="late", tag=last_tag, align_bytes=64)
-        nc.vector.tensor_copy(out=late[:, :H], in_=token_codes[0][:].indirect(offsets_of(3 * C + H, H)))
-        nc.vector.tensor_copy(out=late[:, H:], in_=token_codes[1][:].indirect(offsets_of(3 * C, C)))
-        words2 = gather_tile("words2", "words2", U32, last, 2 * C, C)
-        words3 = gather_tile("words3", "words3", U32, last, 3 * C, C)
+        bytes2 = gather_tile("bytes2", "bytes2", U8, token_bytes, 2 * C, C)
+
+        relu0 = [keep.tile([P, H], F32, name="relu0_0"), keep.tile([P, H], F32, name="relu0_1", tag="relu0_1")]
+        for h in range(2):
+            cols = slice(h * H, (h + 1) * H)
+            nc.scalar.activation(relu0[h][:], accs[h][:], Act.Relu, bias=bias[:, 0:1])
+            nc.scalar.activation(square[:, cols], relu0[h][:], Act.Square)
+        nc.vector.tensor_tensor(gated[:, :C], square[:], gates[:, :C], Alu.mult)
+        relu1 = keep.tile([P, C], F32, name="relu1", tag="relu0_1")
+        bias1 = turns.tile([P, 16], F32, name="bias1", offset=3040)
+        nc.gpsimd.tensor_copy(out=bias1[:, 0:1], in_=bias[:, 1:2])
+        once1 = keep.tile([P, C], F32, name="once1")
+        for h in range(2):
+            cols = slice(h * H, (h + 1) * H)
+            nc.scalar.activation(relu1[:, cols], accs[2 + h][:], Act.Relu, bias=(bias1[:, 0:1], bias[:, 1:2])[h])
+            nc.gpsimd.tensor_tensor(once1[:, cols], relu1[:, cols], gates[:, C + h * H : C + (h + 1) * H], Alu.mult)
+        for h in range(2):
+            cols = slice(h * H, (h + 1) * H)
+            nc.gpsimd.tensor_tensor(gated[:, C + h * H : C + (h + 1) * H], once1[:, cols], relu1[:, cols], Alu.mult)
+
+        bytes3 = turns.tile([P, C], U8, name="bytes3", offset=3072, align_bytes=64)
+        nc.vector.tensor_copy(out=bytes3[:], in_=token_bytes[:].indirect(offsets_of(3 * C, C)))
+        late = turns.tile([P, 3, C], U32, name="late", offset=0, align_bytes=64)
+        nc.vector.tensor_copy(out=late[:, 0, :], in_=token_codes[1][:].indirect(offsets_of(3 * C, C)))
+        nc.vector.tensor_copy(out=late[:, 1, :], in_=last[:].indirect(offsets_of(2 * C, C)))
+        nc.vector.tensor_copy(out=late[:, 2, :], in_=last[:].indirect(offsets_of(3 * C, C)))
         acc2 = psum.tile([P, C], F32, name="acc2")
         acc3 = psum.tile([P, C], F32, name="acc3")
-        one_pass(acc2[:], 2, 0, slot_codes[0][:, 2 * C : 3 * C], bytes23[:, :C])
-        one_pass(acc3[:, :H], 3, 0, slot_codes[0][:, 3 * C :], bytes23[:, C : C + H])
-        one_pass(acc2[:], 2, 1, slot_codes[1][:, 2 * C :], bytes23[:, :C])
-        one_pass(acc3[:, H:], 3, 0, late[:, :H], bytes23[:, C + H :], start=False)
-        one_pass(acc3[:], 3, 1, late[:, H:], bytes23[:, C:])
-        one_pass(acc2[:], 2, 2, words2[:], bytes23[:, :C])
-        one_pass(acc3[:], 3, 2, words3[:], bytes23[:, C:])
+        for a in range(PASSES):
+            one_pass(acc2[:], 2, a, (early_words(2 * C, C) + [late[:, 1, :]])[a], bytes2[:])
+            one_pass(acc3[:], 3, a, (slot_codes[0][:, 3 * C :], late[:, 0, :], late[:, 2, :])[a], bytes3[:])
 
-        relu0 = keep.tile([P, C], F32, name="relu0", tag="relu0")
-        for h in range(2):
-            cols = slice(h * H, (h + 1) * H)
-            nc.scalar.activation(relu0[:, cols], accs[h][:], Act.Relu, bias=bias[:, 0:1])
-            nc.scalar.activation(square[:, cols], relu0[:, cols], Act.Square)
-            nc.gpsimd.tensor_tensor(gated[:, cols], square[:, cols], gates[:, cols], Alu.mult)
-        relu1 = keep.tile([P, C], F32, name="relu1", tag="relu0")
-        for h in range(2):
-            cols = slice(h * H, (h + 1) * H)
-            nc.scalar.activation(relu1[:, cols], accs[2 + h][:], Act.Relu, bias=bias[:, 1:2])
-        gpsimd_product(C, relu1[:])
         relu23 = keep.tile([P, 2 * C], F32, name="relu23")
         once23 = keep.tile([P, 2 * C], F32, name="once23")
         nc.vector.tensor_scalar(relu23[:, :C], acc2[:], bias[:, 2:3], 0.0, Alu.add, Alu.max)

@@ -34,7 +34,7 @@ LAST_PASS_BY_VECTOR = 64
 
 BY_GPSIMD = 256
 
-EARLY_SLOTS = (SLOTS, 3 * C)
+EARLY_SLOTS = (SLOTS, SLOTS)
 
 STORES = (256, 320, 320, 320, 320)
 
@@ -45,7 +45,6 @@ def tile_moe_res_lin_relu2_kernel(tc, xT, xr, w_words, w_scales, b, gate, offs, 
     nc = tc.nc
     with ExitStack() as ctx:
         keep = ctx.enter_context(tc.tile_pool(name="keep", bufs=1))
-        turns = ctx.enter_context(tc.tile_pool(name="turns", bufs=1))
         psum = ctx.enter_context(tc.psum_pool(name="psum", bufs=1))
 
         offsets = keep.tile([P, SLOTS // OFFSETS_PER_COLUMN], U16, name="offsets")
@@ -55,6 +54,8 @@ def tile_moe_res_lin_relu2_kernel(tc, xT, xr, w_words, w_scales, b, gate, offs, 
         gates = keep.tile([P, SLOTS], F32, name="gates")
         resid = keep.tile([P, T], F32, name="resid")
         window = keep.tile([P, T], F32, name="window")
+        window_v = keep.tile([P, T], F32, name="window_v")
+        partial = keep.tile([P, T], F32, name="partial")
         total = keep.tile([P, T], F32, name="total")
         token_codes = [keep.tile([P, T], U32, name=f"token_codes{a}", align_bytes=64) for a in range(PASSES)]
         token_bytes = keep.tile([P, T], U8, name="token_bytes", align_bytes=64)
@@ -64,6 +65,7 @@ def tile_moe_res_lin_relu2_kernel(tc, xT, xr, w_words, w_scales, b, gate, offs, 
         nc.gpsimd.memset(token_bytes[:], 0)
         nc.vector.memset(w_bytes[:].rearrange("p g n -> p (g n)").bitcast(I32), 0)
         nc.vector.memset(window[:], 0.0)
+        nc.vector.memset(window_v[:], 0.0)
 
         rows = [
             xT[a * P * PACK : (a + 1) * P * PACK, :].rearrange("(p r) t -> p r t", r=PACK) for a in range(PASSES)
@@ -128,7 +130,7 @@ def tile_moe_res_lin_relu2_kernel(tc, xT, xr, w_words, w_scales, b, gate, offs, 
             if by_gpsimd:
                 nc.gpsimd.tensor_copy(out=packed[:], in_=raw.rearrange("p r t -> p t r"))
             else:
-                by_vector = (width * FIRST_PASS_SIXTEENTHS // 16, width * 8 // 16, width * 6 // 16)[a]
+                by_vector = (width * FIRST_PASS_SIXTEENTHS // 16, width * 8 // 16, width * 4 // 16)[a]
                 if a == PASSES - 1 and t0 < LAST_LOADS[0]:
                     by_vector = 0
                 else:
@@ -186,45 +188,31 @@ def tile_moe_res_lin_relu2_kernel(tc, xT, xr, w_words, w_scales, b, gate, offs, 
 
         H = C // 2
         last = token_codes[PASSES - 1]
-        gated = keep.tile([P, 2 * C], F32, name="gated")
-        accs = []
-        for e in range(2):
+        gated = [keep.tile([P, C], F32, name=f"gated{e}") for e in range(E - 1)]
+
+        scales0 = gather_tile("bytes0", "bytes0", U8, token_bytes, 0, C)
+        accs0 = []
+        for h in range(2):
+            words = gather_tile(f"words0_{h}", f"words0_{h}", U32, last, h * H, H)
+            accs0.append(multiply(f"acc0_{h}", 0, early_words(h * H, H) + [words[:]], scales0[:, h * H : (h + 1) * H]))
+        accs = [None]
+        for e in range(1, E):
             scales = gather_tile(f"bytes{e}", f"bytes{e}", U8, token_bytes, e * C, C)
-            for h in range(2):
-                j0 = e * C + h * H
-                words = gather_tile(f"words{j0}", f"words{j0}", U32, last, j0, H)
-                accs.append(multiply(f"acc{j0}", e, early_words(j0, H) + [words[:]], scales[:, h * H : (h + 1) * H]))
-        bytes2 = gather_tile("bytes2", "bytes2", U8, token_bytes, 2 * C, C)
+            words = gather_tile(f"words{e}", f"words{e}", U32, last, e * C, C)
+            accs.append(multiply(f"acc{e}", e, early_words(e * C, C) + [words[:]], scales[:]))
+        acc1, acc2, acc3 = accs[1:]
 
-        relu0 = [keep.tile([P, H], F32, name="relu0_0"), keep.tile([P, H], F32, name="relu0_1", tag="relu0_1")]
+        relu0 = keep.tile([P, C], F32, name="relu0")
         for h in range(2):
             cols = slice(h * H, (h + 1) * H)
-            nc.scalar.activation(relu0[h][:], accs[h][:], Act.Relu, bias=bias[:, 0:1])
-            nc.scalar.activation(square[:, cols], relu0[h][:], Act.Square)
-        nc.vector.tensor_tensor(gated[:, :C], square[:], gates[:, :C], Alu.mult)
-        relu1 = keep.tile([P, C], F32, name="relu1", tag="relu0_1")
-        bias1 = turns.tile([P, 16], F32, name="bias1", offset=3040)
-        nc.gpsimd.tensor_copy(out=bias1[:, 0:1], in_=bias[:, 1:2])
+            nc.scalar.activation(relu0[:, cols], accs0[h][:], Act.Relu, bias=bias[:, 0:1])
+            nc.scalar.activation(square[:, cols], relu0[:, cols], Act.Square)
+            nc.gpsimd.tensor_tensor(gated[0][:, cols], square[:, cols], gates[:, cols], Alu.mult)
+        relu1 = keep.tile([P, C], F32, name="relu1")
         once1 = keep.tile([P, C], F32, name="once1")
-        for h in range(2):
-            cols = slice(h * H, (h + 1) * H)
-            nc.scalar.activation(relu1[:, cols], accs[2 + h][:], Act.Relu, bias=(bias1[:, 0:1], bias[:, 1:2])[h])
-            nc.gpsimd.tensor_tensor(once1[:, cols], relu1[:, cols], gates[:, C + h * H : C + (h + 1) * H], Alu.mult)
-        for h in range(2):
-            cols = slice(h * H, (h + 1) * H)
-            nc.gpsimd.tensor_tensor(gated[:, C + h * H : C + (h + 1) * H], once1[:, cols], relu1[:, cols], Alu.mult)
-
-        bytes3 = turns.tile([P, C], U8, name="bytes3", offset=3072, align_bytes=64)
-        nc.vector.tensor_copy(out=bytes3[:], in_=token_bytes[:].indirect(offsets_of(3 * C, C)))
-        late = turns.tile([P, 3, C], U32, name="late", offset=0, align_bytes=64)
-        nc.vector.tensor_copy(out=late[:, 0, :], in_=token_codes[1][:].indirect(offsets_of(3 * C, C)))
-        nc.vector.tensor_copy(out=late[:, 1, :], in_=last[:].indirect(offsets_of(2 * C, C)))
-        nc.vector.tensor_copy(out=late[:, 2, :], in_=last[:].indirect(offsets_of(3 * C, C)))
-        acc2 = psum.tile([P, C], F32, name="acc2")
-        acc3 = psum.tile([P, C], F32, name="acc3")
-        for a in range(PASSES):
-            one_pass(acc2[:], 2, a, (early_words(2 * C, C) + [late[:, 1, :]])[a], bytes2[:])
-            one_pass(acc3[:], 3, a, (slot_codes[0][:, 3 * C :], late[:, 0, :], late[:, 2, :])[a], bytes3[:])
+        nc.scalar.activation(relu1[:], acc1[:], Act.Relu, bias=bias[:, 1:2])
+        nc.gpsimd.tensor_tensor(once1[:], relu1[:], gates[:, C : 2 * C], Alu.mult)
+        nc.gpsimd.tensor_tensor(gated[1][:], once1[:], relu1[:], Alu.mult)
 
         relu23 = keep.tile([P, 2 * C], F32, name="relu23")
         once23 = keep.tile([P, 2 * C], F32, name="once23")
@@ -232,13 +220,15 @@ def tile_moe_res_lin_relu2_kernel(tc, xT, xr, w_words, w_scales, b, gate, offs, 
         nc.vector.scalar_tensor_tensor(once23[:, :C], acc2[:], bias[:, 2:3], gates[:, 2 * C : 3 * C], Alu.add, Alu.mult)
         nc.vector.tensor_scalar(relu23[:, C:], acc3[:], bias[:, 3:4], 0.0, Alu.add, Alu.max)
         nc.vector.scalar_tensor_tensor(once23[:, C:], acc3[:], bias[:, 3:4], gates[:, 3 * C :], Alu.add, Alu.mult)
+        nc.vector.tensor_tensor(gated[2][:], relu23[:, :C], once23[:, :C], Alu.mult)
 
-        for e in range(2):
-            nc.scalar.activation(window[:].indirect(offsets_of(e * C, C)), gated[:, e * C : (e + 1) * C], Act.Copy)
-        nc.vector.tensor_tensor(window[:].indirect(offsets_of(2 * C, 2 * C)), relu23[:], once23[:], Alu.mult)
+        for e in range(E - 1):
+            nc.scalar.activation(window[:].indirect(offsets_of(e * C, C)), gated[e][:], Act.Copy)
+        nc.vector.tensor_tensor(window_v[:].indirect(offsets_of(3 * C, C)), relu23[:, C:], once23[:, C:], Alu.mult)
+        nc.vector.tensor_tensor(partial[:], window_v[:], resid[:], Alu.add)
         t0 = 0
         for width in STORES:
             cols = slice(t0, t0 + width)
-            nc.vector.tensor_tensor(total[:, cols], window[:, cols], resid[:, cols], Alu.add)
+            nc.vector.tensor_tensor(total[:, cols], window[:, cols], partial[:, cols], Alu.add)
             nc.sync.dma_start(out=out[:, cols], in_=total[:, cols])
             t0 += width

@@ -60,7 +60,7 @@ def tile_moe_res_lin_relu2_kernel(tc, xT, xr, w_words, w_scales, b, gate, offs, 
         token_codes = [keep.tile([P, T], U32, name=f"token_codes{a}", align_bytes=64) for a in range(PASSES)]
         token_bytes = keep.tile([P, T], U8, name="token_bytes", align_bytes=64)
         slot_codes = [keep.tile([P, EARLY_SLOTS[a]], U32, name=f"slot_codes{a}", align_bytes=64) for a in range(PASSES - 1)]
-        square = keep.tile([P, C], F32, name="square")
+        square = keep.tile([P, C], F32, name="square", tag="square")
 
         nc.gpsimd.memset(token_bytes[:], 0)
         nc.vector.memset(w_bytes[:].rearrange("p g n -> p (g n)").bitcast(I32), 0)
@@ -112,8 +112,8 @@ def tile_moe_res_lin_relu2_kernel(tc, xT, xr, w_words, w_scales, b, gate, offs, 
         nc.sync.dma_start(out=bias[:], in_=b)
         load_weights(1, 1)
         nc.sync.dma_start(out=gates[:, :C], in_=gate[:, :C])
-        nc.sync.dma_start(out=gates[:, C:], in_=gate[:, C:])
         load_weights(2, 2)
+        nc.sync.dma_start(out=gates[:, C:], in_=gate[:, C:])
         nc.sync.dma_start(out=resid[:], in_=xr)
 
         def by_runs(raw, i0, i1):
@@ -195,12 +195,12 @@ def tile_moe_res_lin_relu2_kernel(tc, xT, xr, w_words, w_scales, b, gate, offs, 
         for h in range(2):
             words = gather_tile(f"words0_{h}", f"words0_{h}", U32, last, h * H, H)
             accs0.append(multiply(f"acc0_{h}", 0, early_words(h * H, H) + [words[:]], scales0[:, h * H : (h + 1) * H]))
-        accs = [None]
-        for e in range(1, E):
+        accs = {}
+        for e in (1, 3, 2):
             scales = gather_tile(f"bytes{e}", f"bytes{e}", U8, token_bytes, e * C, C)
             words = gather_tile(f"words{e}", f"words{e}", U32, last, e * C, C)
-            accs.append(multiply(f"acc{e}", e, early_words(e * C, C) + [words[:]], scales[:]))
-        acc1, acc2, acc3 = accs[1:]
+            accs[e] = multiply(f"acc{e}", e, early_words(e * C, C) + [words[:]], scales[:])
+        acc1, acc2, acc3 = accs[1], accs[2], accs[3]
 
         relu0 = keep.tile([P, C], F32, name="relu0")
         for h in range(2):
@@ -214,17 +214,22 @@ def tile_moe_res_lin_relu2_kernel(tc, xT, xr, w_words, w_scales, b, gate, offs, 
         nc.gpsimd.tensor_tensor(once1[:], relu1[:], gates[:, C : 2 * C], Alu.mult)
         nc.gpsimd.tensor_tensor(gated[1][:], once1[:], relu1[:], Alu.mult)
 
-        relu23 = keep.tile([P, 2 * C], F32, name="relu23")
-        once23 = keep.tile([P, 2 * C], F32, name="once23")
-        nc.vector.tensor_scalar(relu23[:, :C], acc2[:], bias[:, 2:3], 0.0, Alu.add, Alu.max)
-        nc.vector.scalar_tensor_tensor(once23[:, :C], acc2[:], bias[:, 2:3], gates[:, 2 * C : 3 * C], Alu.add, Alu.mult)
-        nc.vector.tensor_scalar(relu23[:, C:], acc3[:], bias[:, 3:4], 0.0, Alu.add, Alu.max)
-        nc.vector.scalar_tensor_tensor(once23[:, C:], acc3[:], bias[:, 3:4], gates[:, 3 * C :], Alu.add, Alu.mult)
-        nc.vector.tensor_tensor(gated[2][:], relu23[:, :C], once23[:, :C], Alu.mult)
+        relu3 = keep.tile([P, C], F32, name="relu3")
+        square3 = keep.tile([P, C], F32, name="square3")
+        gated3 = keep.tile([P, C], F32, name="gated3")
+        nc.vector.tensor_scalar(relu3[:], acc3[:], bias[:, 3:4], 0.0, Alu.add, Alu.max)
+        nc.vector.scalar_tensor_tensor(square3[:], acc3[:], bias[:, 3:4], relu3[:], Alu.add, Alu.mult)
+        nc.vector.tensor_tensor(gated3[:], square3[:], gates[:, 3 * C :], Alu.mult)
+        nc.vector.tensor_copy(out=window_v[:].indirect(offsets_of(3 * C, C)), in_=gated3[:])
 
-        for e in range(E - 1):
+        nc.scalar.activation(window[:].indirect(offsets_of(0, C)), gated[0][:], Act.Copy)
+        relu2 = keep.tile([P, C], F32, name="relu2", tag="square")
+        once2 = keep.tile([P, C], F32, name="once2")
+        nc.scalar.activation(relu2[:], acc2[:], Act.Relu, bias=bias[:, 2:3])
+        nc.gpsimd.tensor_tensor(once2[:], relu2[:], gates[:, 2 * C : 3 * C], Alu.mult)
+        nc.gpsimd.tensor_tensor(gated[2][:], once2[:], relu2[:], Alu.mult)
+        for e in range(1, E - 1):
             nc.scalar.activation(window[:].indirect(offsets_of(e * C, C)), gated[e][:], Act.Copy)
-        nc.vector.tensor_tensor(window_v[:].indirect(offsets_of(3 * C, C)), relu23[:, C:], once23[:, C:], Alu.mult)
         nc.vector.tensor_tensor(partial[:], window_v[:], resid[:], Alu.add)
         t0 = 0
         for width in STORES:

@@ -22,23 +22,12 @@ FP8X4 = mybir.dt.float8_e4m3fn_x4
 Act = mybir.ActivationFunctionType
 Alu = mybir.AluOpType
 
-LAST_LOADS = (640, 512, 256, 128)
-LOADS = ((3, (T,)), (3, (768, 768)), (0, LAST_LOADS))
+BY_VECTOR = (512, 512, 384)
+CHUNKS = (((0, 512), (512, 512)), ((0, 512), (512, 512)), ((0, 384), (384, 384), (768, 256)))
 
-CHUNKS = (512, 256, 128)
-LAST_CHUNKS = (384, 256, 128)
-PLANES = (8, 4, 0)
-
-FIRST_PASS_SIXTEENTHS = 9
-LAST_PASS_BY_VECTOR = 64
-
-BY_GPSIMD = 256
-
-EARLY_SLOTS = (SLOTS, SLOTS)
+ROWS_BEFORE_WEIGHTS = 10
 
 STORES = (256, 320, 320, 320, 320)
-
-RUN = 2
 
 
 def tile_moe_res_lin_relu2_kernel(tc, xT, xr, w_words, w_scales, b, gate, offs, out):
@@ -53,48 +42,16 @@ def tile_moe_res_lin_relu2_kernel(tc, xT, xr, w_words, w_scales, b, gate, offs, 
         bias = keep.tile([P, E], F32, name="bias")
         gates = keep.tile([P, SLOTS], F32, name="gates")
         resid = keep.tile([P, T], F32, name="resid")
-        window = keep.tile([P, T], F32, name="window")
+        window_s = keep.tile([P, T], F32, name="window_s")
         window_v = keep.tile([P, T], F32, name="window_v")
         partial = keep.tile([P, T], F32, name="partial")
         total = keep.tile([P, T], F32, name="total")
-        token_codes = [keep.tile([P, T], U32, name=f"token_codes{a}", align_bytes=64) for a in range(PASSES)]
-        token_bytes = keep.tile([P, T], U8, name="token_bytes", align_bytes=64)
-        slot_codes = [keep.tile([P, EARLY_SLOTS[a]], U32, name=f"slot_codes{a}", align_bytes=64) for a in range(PASSES - 1)]
-        square = keep.tile([P, C], F32, name="square", tag="square")
+        codes = [keep.tile([P, SLOTS], U32, name=f"codes{a}", align_bytes=64) for a in range(PASSES)]
+        scales = [keep.tile([P, SLOTS], U8, name=f"scales{a}", align_bytes=64) for a in range(PASSES)]
 
-        nc.gpsimd.memset(token_bytes[:], 0)
         nc.vector.memset(w_bytes[:].rearrange("p g n -> p (g n)").bitcast(I32), 0)
-        nc.vector.memset(window[:], 0.0)
         nc.vector.memset(window_v[:], 0.0)
-
-        rows = [
-            xT[a * P * PACK : (a + 1) * P * PACK, :].rearrange("(p r) t -> p r t", r=PACK) for a in range(PASSES)
-        ]
-        pieces = [[] for a in range(PASSES)]
-        for a in range(PASSES):
-            whole, widths = LOADS[a]
-            if whole == 0:
-                t0 = 0
-                for width in widths:
-                    raw = keep.tile([P, PACK, width], F32, name=f"raw{a}_{t0}")
-                    nc.sync.dma_start(out=raw[:], in_=rows[a][:, :, t0 : t0 + width])
-                    pieces[a].append((t0, width, raw[:]))
-                    t0 += width
-                continue
-            raw = keep.tile([P, PACK, T], F32, name=f"raw{a}")
-            run = whole * T + widths[0]
-            nc.sync.dma_start(
-                out=raw[:].rearrange("p r t -> p (r t)")[:, :run], in_=rows[a].rearrange("p r t -> p (r t)")[:, :run]
-            )
-            if a == 0:
-                nc.sync.dma_start(offsets[:], offs)
-            t0 = 0
-            for width in widths:
-                cols = slice(t0, t0 + width)
-                if t0 > 0:
-                    nc.sync.dma_start(out=raw[:, whole:, cols], in_=rows[a][:, whole:, cols])
-                pieces[a].append((t0, width, raw[:, :, cols]))
-                t0 += width
+        nc.scalar.activation(window_s[:], window_v[:], Act.Copy)
 
         def load_weights(e, experts):
             nc.sync.dma_start(
@@ -102,138 +59,98 @@ def tile_moe_res_lin_relu2_kernel(tc, xT, xr, w_words, w_scales, b, gate, offs, 
                 in_=w_words[e : e + experts].rearrange("e a p n r -> p (e a) (n r)").bitcast(I32),
             )
 
-        load_weights(0, 1)
-        for q in range(SCALE_ROWS):
-            nc.sync.dma_start(
-                out=w_bytes[q:P:32, :, :].bitcast(I32),
-                in_=w_scales[:, :, q:16:SCALE_ROWS, :].rearrange("e a q n -> q (e a) n").bitcast(I32),
-            )
-
+        rows = []
+        for a in range(PASSES):
+            of_pass = xT[a * P * PACK : (a + 1) * P * PACK, :].rearrange("(p r) t -> p r t", r=PACK)
+            for r in range(PACK):
+                if len(rows) == ROWS_BEFORE_WEIGHTS:
+                    load_weights(0, 2)
+                    load_weights(2, 2)
+                    for q in range(SCALE_ROWS):
+                        nc.sync.dma_start(
+                            out=w_bytes[q:P:32, :, :].bitcast(I32),
+                            in_=w_scales[:, :, q:16:SCALE_ROWS, :].rearrange("e a q n -> q (e a) n").bitcast(I32),
+                        )
+                row = keep.tile([P, T], F32, name=f"row{a}_{r}")
+                nc.sync.dma_start(out=row[:], in_=of_pass[:, r, :])
+                rows.append(row)
+                if a == 0 and r == 0:
+                    nc.sync.dma_start(offsets[:], offs)
         nc.sync.dma_start(out=bias[:], in_=b)
-        load_weights(1, 1)
         nc.sync.dma_start(out=gates[:, :C], in_=gate[:, :C])
-        load_weights(2, 2)
         nc.sync.dma_start(out=gates[:, C:], in_=gate[:, C:])
         nc.sync.dma_start(out=resid[:], in_=xr)
-
-        def by_runs(raw, i0, i1):
-            return raw[:, :, i0:i1].rearrange("p r (c i) -> p c r i", i=RUN)
-
-        def interleaved(packed, i0, i1):
-            return packed[:, i0:i1, :].rearrange("p (c i) r -> p c r i", i=RUN)
-
-        def round_and_quantise(a, t0, width, raw):
-            by_gpsimd = a == PASSES - 1 and t0 == 0
-            last_before_gather = a == PASSES - 2 and t0 + width == T
-            tag = "beside_gather" if by_gpsimd or last_before_gather else f"packed{a}_{t0}"
-            packed = keep.tile([P, width, PACK], BF16, name=f"packed{a}_{t0}", tag=tag, align_bytes=64)
-            if by_gpsimd:
-                nc.gpsimd.tensor_copy(out=packed[:], in_=raw.rearrange("p r t -> p t r"))
-            else:
-                by_vector = (width * FIRST_PASS_SIXTEENTHS // 16, width * 8 // 16, width * 4 // 16)[a]
-                if a == PASSES - 1 and t0 < LAST_LOADS[0]:
-                    by_vector = 0
-                else:
-                    nc.vector.tensor_copy(out=interleaved(packed, 0, by_vector), in_=by_runs(raw, 0, by_vector))
-                nc.scalar.activation(interleaved(packed, by_vector, width), by_runs(raw, by_vector, width), Act.Copy)
-            nc.vector.quantize_mx(
-                out=token_codes[a][:, t0 : t0 + width].bitcast(FP8X4),
-                scales=token_bytes[PLANES[a] : P, t0 : t0 + width],
-                in_=packed[:].rearrange("p t r -> p (t r)"),
-            )
 
         def offsets_of(j0, slots):
             return offsets[:, j0 // OFFSETS_PER_COLUMN : (j0 + slots) // OFFSETS_PER_COLUMN]
 
-        def gather(of_slots, of_tokens, j0, slots):
-            nc.vector.tensor_copy(out=of_slots[:, j0 : j0 + slots], in_=of_tokens[:].indirect(offsets_of(j0, slots)))
-
         for a in range(PASSES):
-            for t0, width, raw in pieces[a]:
-                i0 = 0
-                while i0 < width:
-                    if a == PASSES - 1 and t0 + i0 == 0:
-                        chunk = BY_GPSIMD
-                    else:
-                        chunk = max(c for c in (LAST_CHUNKS if a == PASSES - 1 else CHUNKS) if c <= width - i0 and width - i0 - c != P)
-                    round_and_quantise(a, t0 + i0, chunk, raw[:, :, i0 : i0 + chunk])
-                    i0 += chunk
-            if a < PASSES - 1:
-                gather(slot_codes[a], token_codes[a], 0, EARLY_SLOTS[a])
+            split = BY_VECTOR[a]
+            packed_v = keep.tile([P, split, PACK], BF16, name=f"packed_v{a}", align_bytes=64)
+            packed_s = keep.tile([P, SLOTS - split, PACK], BF16, name=f"packed_s{a}", align_bytes=64)
+            for r in range(PACK):
+                row = rows[a * PACK + r]
+                nc.vector.tensor_copy(out=packed_v[:, :, r], in_=row[:].indirect(offsets_of(0, split)))
+                parts = CHUNKS[a][1:] if r == PACK - 1 else ((split, SLOTS - split),)
+                for j0, slots in parts:
+                    nc.scalar.activation(
+                        packed_s[:, j0 - split : j0 - split + slots, r], row[:].indirect(offsets_of(j0, slots)), Act.Copy
+                    )
+            for j0, slots in CHUNKS[a]:
+                source = packed_v[:] if j0 == 0 else packed_s[:, j0 - split : j0 - split + slots, :]
+                nc.vector.quantize_mx(
+                    out=codes[a][:, j0 : j0 + slots].bitcast(FP8X4),
+                    scales=scales[a][:, j0 : j0 + slots],
+                    in_=source.rearrange("p t r -> p (t r)"),
+                )
 
-        def gather_tile(name, tag, dtype, of_tokens, j0, slots):
-            tile = keep.tile([P, slots], dtype, name=name, tag=tag, align_bytes=64)
-            nc.vector.tensor_copy(out=tile[:], in_=of_tokens[:].indirect(offsets_of(j0, slots)))
-            return tile
+        accs = [psum.tile([P, C], F32, name=f"acc{e}") for e in range(E)]
+        for a in range(PASSES):
+            for e in range(E):
+                cols = slice(e * C, (e + 1) * C)
+                nc.tensor.matmul_mx(
+                    out=accs[e][:],
+                    lhsT=w_codes[:, e * PASSES + a, :].bitcast(FP8X4),
+                    lhsT_scale=w_bytes[:, e * PASSES + a, :],
+                    rhs=codes[a][:, cols].bitcast(FP8X4),
+                    rhs_scale=scales[a][:, cols],
+                    start=(a == 0),
+                    stop=(a == PASSES - 1),
+                )
 
-        def one_pass(acc, e, a, words, scales, start=True):
-            nc.tensor.matmul_mx(
-                out=acc,
-                lhsT=w_codes[:, e * PASSES + a, :].bitcast(FP8X4),
-                lhsT_scale=w_bytes[:, e * PASSES + a, :],
-                rhs=words.bitcast(FP8X4),
-                rhs_scale=scales[PLANES[a] : P, :],
-                start=start and a == 0,
-                stop=(a == PASSES - 1),
+        relus = [keep.tile([P, C], F32, name=f"relu{e}") for e in range(E)]
+        squares = [keep.tile([P, C], F32, name=f"square{e}") for e in range(E)]
+
+        def relu(e):
+            nc.scalar.activation(relus[e][:], accs[e][:], Act.Relu, bias=bias[:, e : e + 1])
+
+        def square(e):
+            nc.scalar.activation(squares[e][:], relus[e][:], Act.Square)
+
+        def scatter_by_vector(e):
+            nc.vector.tensor_tensor(
+                window_v[:].indirect(offsets_of(e * C, C)), squares[e][:], gates[:, e * C : (e + 1) * C], Alu.mult
             )
 
-        def multiply(name, e, words, scales):
-            acc = psum.tile([P, words[0].shape[1]], F32, name=name)
-            for a in range(PASSES):
-                one_pass(acc[:], e, a, words[a], scales)
-            return acc
+        relu(0)
+        square(0)
+        relu(1)
+        for e in range(2, E):
+            relu(e)
+            square(e - 1)
+        square(E - 1)
 
-        def early_words(j0, slots):
-            return [slot_codes[a][:, j0 : j0 + slots] for a in range(PASSES - 1)]
+        scatter_by_vector(0)
+        for e in (1, 2):
+            gated = keep.tile([P, C], F32, name=f"gated{e}")
+            nc.vector.tensor_tensor(gated[:], squares[e][:], gates[:, e * C : (e + 1) * C], Alu.mult)
+            nc.scalar.activation(window_s[:].indirect(offsets_of(e * C, C)), gated[:], Act.Copy)
+        scatter_by_vector(3)
 
-        H = C // 2
-        last = token_codes[PASSES - 1]
-        gated = [keep.tile([P, C], F32, name=f"gated{e}") for e in range(E - 1)]
-
-        scales0 = gather_tile("bytes0", "bytes0", U8, token_bytes, 0, C)
-        accs0 = []
-        for h in range(2):
-            words = gather_tile(f"words0_{h}", f"words0_{h}", U32, last, h * H, H)
-            accs0.append(multiply(f"acc0_{h}", 0, early_words(h * H, H) + [words[:]], scales0[:, h * H : (h + 1) * H]))
-        accs = {}
-        for e in (1, 3, 2):
-            scales = gather_tile(f"bytes{e}", f"bytes{e}", U8, token_bytes, e * C, C)
-            words = gather_tile(f"words{e}", f"words{e}", U32, last, e * C, C)
-            accs[e] = multiply(f"acc{e}", e, early_words(e * C, C) + [words[:]], scales[:])
-        acc1, acc2, acc3 = accs[1], accs[2], accs[3]
-
-        relu0 = keep.tile([P, C], F32, name="relu0")
-        for h in range(2):
-            cols = slice(h * H, (h + 1) * H)
-            nc.scalar.activation(relu0[:, cols], accs0[h][:], Act.Relu, bias=bias[:, 0:1])
-            nc.scalar.activation(square[:, cols], relu0[:, cols], Act.Square)
-            nc.gpsimd.tensor_tensor(gated[0][:, cols], square[:, cols], gates[:, cols], Alu.mult)
-        relu1 = keep.tile([P, C], F32, name="relu1")
-        once1 = keep.tile([P, C], F32, name="once1")
-        nc.scalar.activation(relu1[:], acc1[:], Act.Relu, bias=bias[:, 1:2])
-        nc.gpsimd.tensor_tensor(once1[:], relu1[:], gates[:, C : 2 * C], Alu.mult)
-        nc.gpsimd.tensor_tensor(gated[1][:], once1[:], relu1[:], Alu.mult)
-
-        relu3 = keep.tile([P, C], F32, name="relu3")
-        square3 = keep.tile([P, C], F32, name="square3")
-        gated3 = keep.tile([P, C], F32, name="gated3")
-        nc.vector.tensor_scalar(relu3[:], acc3[:], bias[:, 3:4], 0.0, Alu.add, Alu.max)
-        nc.vector.scalar_tensor_tensor(square3[:], acc3[:], bias[:, 3:4], relu3[:], Alu.add, Alu.mult)
-        nc.vector.tensor_tensor(gated3[:], square3[:], gates[:, 3 * C :], Alu.mult)
-        nc.vector.tensor_copy(out=window_v[:].indirect(offsets_of(3 * C, C)), in_=gated3[:])
-
-        nc.scalar.activation(window[:].indirect(offsets_of(0, C)), gated[0][:], Act.Copy)
-        relu2 = keep.tile([P, C], F32, name="relu2", tag="square")
-        once2 = keep.tile([P, C], F32, name="once2")
-        nc.scalar.activation(relu2[:], acc2[:], Act.Relu, bias=bias[:, 2:3])
-        nc.gpsimd.tensor_tensor(once2[:], relu2[:], gates[:, 2 * C : 3 * C], Alu.mult)
-        nc.gpsimd.tensor_tensor(gated[2][:], once2[:], relu2[:], Alu.mult)
-        for e in range(1, E - 1):
-            nc.scalar.activation(window[:].indirect(offsets_of(e * C, C)), gated[e][:], Act.Copy)
         nc.vector.tensor_tensor(partial[:], window_v[:], resid[:], Alu.add)
         t0 = 0
         for width in STORES:
             cols = slice(t0, t0 + width)
-            nc.vector.tensor_tensor(total[:, cols], window[:, cols], partial[:, cols], Alu.add)
+            nc.vector.tensor_tensor(total[:, cols], window_s[:, cols], partial[:, cols], Alu.add)
             nc.sync.dma_start(out=out[:, cols], in_=total[:, cols])
             t0 += width

@@ -22,10 +22,8 @@ FP8X4 = mybir.dt.float8_e4m3fn_x4
 Act = mybir.ActivationFunctionType
 Alu = mybir.AluOpType
 
-BY_VECTOR = (512, 512, 384)
-CHUNKS = (((0, 512), (512, 512)), ((0, 512), (512, 512)), ((0, 384), (384, 384), (768, 256)))
-
-ROWS_BEFORE_WEIGHTS = 10
+BY_VECTOR = (512, 512, 512)
+CHUNKS = (((0, 512), (512, 512)), ((0, 512), (512, 512)), ((0, 256), (512, 256), (256, 256), (768, 256)))
 
 STORES = (256, 320, 320, 320, 320)
 
@@ -63,21 +61,22 @@ def tile_moe_res_lin_relu2_kernel(tc, xT, xr, w_words, w_scales, b, gate, offs, 
         for a in range(PASSES):
             of_pass = xT[a * P * PACK : (a + 1) * P * PACK, :].rearrange("(p r) t -> p r t", r=PACK)
             for r in range(PACK):
-                if len(rows) == ROWS_BEFORE_WEIGHTS:
-                    load_weights(0, 2)
-                    load_weights(2, 2)
-                    for q in range(SCALE_ROWS):
-                        nc.sync.dma_start(
-                            out=w_bytes[q:P:32, :, :].bitcast(I32),
-                            in_=w_scales[:, :, q:16:SCALE_ROWS, :].rearrange("e a q n -> q (e a) n").bitcast(I32),
-                        )
                 row = keep.tile([P, T], F32, name=f"row{a}_{r}")
                 nc.sync.dma_start(out=row[:], in_=of_pass[:, r, :])
                 rows.append(row)
                 if a == 0 and r == 0:
                     nc.sync.dma_start(offsets[:], offs)
+        for q in range(SCALE_ROWS):
+            nc.sync.dma_start(
+                out=w_bytes[q:P:32, :, :].bitcast(I32),
+                in_=w_scales[:, :, q:16:SCALE_ROWS, :].rearrange("e a q n -> q (e a) n").bitcast(I32),
+            )
+        load_weights(0, 1)
         nc.sync.dma_start(out=bias[:], in_=b)
+        load_weights(2, 1)
         nc.sync.dma_start(out=gates[:, :C], in_=gate[:, :C])
+        load_weights(1, 1)
+        load_weights(3, 1)
         nc.sync.dma_start(out=gates[:, C:], in_=gate[:, C:])
         nc.sync.dma_start(out=resid[:], in_=xr)
 
@@ -90,14 +89,15 @@ def tile_moe_res_lin_relu2_kernel(tc, xT, xr, w_words, w_scales, b, gate, offs, 
             packed_s = keep.tile([P, SLOTS - split, PACK], BF16, name=f"packed_s{a}", align_bytes=64)
             for r in range(PACK):
                 row = rows[a * PACK + r]
-                nc.vector.tensor_copy(out=packed_v[:, :, r], in_=row[:].indirect(offsets_of(0, split)))
-                parts = CHUNKS[a][1:] if r == PACK - 1 else ((split, SLOTS - split),)
+                parts = CHUNKS[a] if r == PACK - 1 else ((0, split), (split, SLOTS - split))
                 for j0, slots in parts:
-                    nc.scalar.activation(
-                        packed_s[:, j0 - split : j0 - split + slots, r], row[:].indirect(offsets_of(j0, slots)), Act.Copy
-                    )
+                    picked = row[:].indirect(offsets_of(j0, slots))
+                    if j0 < split:
+                        nc.vector.tensor_copy(out=packed_v[:, j0 : j0 + slots, r], in_=picked)
+                    else:
+                        nc.scalar.activation(packed_s[:, j0 - split : j0 - split + slots, r], picked, Act.Copy)
             for j0, slots in CHUNKS[a]:
-                source = packed_v[:] if j0 == 0 else packed_s[:, j0 - split : j0 - split + slots, :]
+                source = packed_v[:, j0 : j0 + slots, :] if j0 < split else packed_s[:, j0 - split : j0 - split + slots, :]
                 nc.vector.quantize_mx(
                     out=codes[a][:, j0 : j0 + slots].bitcast(FP8X4),
                     scales=scales[a][:, j0 : j0 + slots],
@@ -106,7 +106,7 @@ def tile_moe_res_lin_relu2_kernel(tc, xT, xr, w_words, w_scales, b, gate, offs, 
 
         accs = [psum.tile([P, C], F32, name=f"acc{e}") for e in range(E)]
         for a in range(PASSES):
-            for e in range(E):
+            for e in (0, 2, 1, 3):
                 cols = slice(e * C, (e + 1) * C)
                 nc.tensor.matmul_mx(
                     out=accs[e][:],
@@ -132,16 +132,12 @@ def tile_moe_res_lin_relu2_kernel(tc, xT, xr, w_words, w_scales, b, gate, offs, 
                 window_v[:].indirect(offsets_of(e * C, C)), squares[e][:], gates[:, e * C : (e + 1) * C], Alu.mult
             )
 
-        relu(0)
-        square(0)
-        relu(1)
-        for e in range(2, E):
+        for e in (0, 2, 1, 3):
             relu(e)
-            square(e - 1)
-        square(E - 1)
+            square(e)
 
         scatter_by_vector(0)
-        for e in (1, 2):
+        for e in (2, 1):
             gated = keep.tile([P, C], F32, name=f"gated{e}")
             nc.vector.tensor_tensor(gated[:], squares[e][:], gates[:, e * C : (e + 1) * C], Alu.mult)
             nc.scalar.activation(window_s[:].indirect(offsets_of(e * C, C)), gated[:], Act.Copy)

@@ -22,8 +22,8 @@ FP8X4 = mybir.dt.float8_e4m3fn_x4
 Act = mybir.ActivationFunctionType
 Alu = mybir.AluOpType
 
-BY_VECTOR = (512, 512, 512)
-CHUNKS = (((0, 512), (512, 512)), ((0, 512), (512, 512)), ((0, 256), (512, 256), (256, 256), (768, 256)))
+BY_VECTOR = (512, 480, 416)
+ORDER = (0, 3, 1, 2)
 
 STORES = (256, 320, 320, 320, 320)
 
@@ -71,42 +71,45 @@ def tile_moe_res_lin_relu2_kernel(tc, xT, xr, w_words, w_scales, b, gate, offs, 
                 out=w_bytes[q:P:32, :, :].bitcast(I32),
                 in_=w_scales[:, :, q:16:SCALE_ROWS, :].rearrange("e a q n -> q (e a) n").bitcast(I32),
             )
-        load_weights(0, 1)
+        load_weights(ORDER[0], 1)
         nc.sync.dma_start(out=bias[:], in_=b)
-        load_weights(2, 1)
+        load_weights(ORDER[1], 1)
         nc.sync.dma_start(out=gates[:, :C], in_=gate[:, :C])
-        load_weights(1, 1)
-        load_weights(3, 1)
+        load_weights(ORDER[2], 1)
+        load_weights(ORDER[3], 1)
         nc.sync.dma_start(out=gates[:, C:], in_=gate[:, C:])
         nc.sync.dma_start(out=resid[:], in_=xr)
 
         def offsets_of(j0, slots):
             return offsets[:, j0 // OFFSETS_PER_COLUMN : (j0 + slots) // OFFSETS_PER_COLUMN]
 
+        def quantise(a, packed, j0, slots):
+            nc.vector.quantize_mx(
+                out=codes[a][:, j0 : j0 + slots].bitcast(FP8X4),
+                scales=scales[a][:, j0 : j0 + slots],
+                in_=packed[:, j0 : j0 + slots, :].rearrange("p t r -> p (t r)"),
+            )
+
         for a in range(PASSES):
-            split = BY_VECTOR[a]
-            packed_v = keep.tile([P, split, PACK], BF16, name=f"packed_v{a}", align_bytes=64)
-            packed_s = keep.tile([P, SLOTS - split, PACK], BF16, name=f"packed_s{a}", align_bytes=64)
+            split = SLOTS - BY_VECTOR[a]
+            packed = keep.tile([P, SLOTS, PACK], BF16, name=f"packed{a}", align_bytes=64)
             for r in range(PACK):
                 row = rows[a * PACK + r]
-                parts = CHUNKS[a] if r == PACK - 1 else ((0, split), (split, SLOTS - split))
-                for j0, slots in parts:
-                    picked = row[:].indirect(offsets_of(j0, slots))
-                    if j0 < split:
-                        nc.vector.tensor_copy(out=packed_v[:, j0 : j0 + slots, r], in_=picked)
-                    else:
-                        nc.scalar.activation(packed_s[:, j0 - split : j0 - split + slots, r], picked, Act.Copy)
-            for j0, slots in CHUNKS[a]:
-                source = packed_v[:, j0 : j0 + slots, :] if j0 < split else packed_s[:, j0 - split : j0 - split + slots, :]
-                nc.vector.quantize_mx(
-                    out=codes[a][:, j0 : j0 + slots].bitcast(FP8X4),
-                    scales=scales[a][:, j0 : j0 + slots],
-                    in_=source.rearrange("p t r -> p (t r)"),
-                )
+                nc.vector.tensor_copy(out=packed[:, split:, r], in_=row[:].indirect(offsets_of(split, SLOTS - split)))
+                ends = (C, split) if a == PASSES - 1 and r == PACK - 1 else (split,)
+                j0 = 0
+                for j1 in ends:
+                    nc.scalar.activation(packed[:, j0:j1, r], row[:].indirect(offsets_of(j0, j1 - j0)), Act.Copy)
+                    j0 = j1
+            if a < PASSES - 1:
+                quantise(a, packed, 0, SLOTS)
+            else:
+                for e in ORDER:
+                    quantise(a, packed, e * C, C)
 
         accs = [psum.tile([P, C], F32, name=f"acc{e}") for e in range(E)]
         for a in range(PASSES):
-            for e in (0, 2, 1, 3):
+            for e in ORDER:
                 cols = slice(e * C, (e + 1) * C)
                 nc.tensor.matmul_mx(
                     out=accs[e][:],
@@ -132,16 +135,16 @@ def tile_moe_res_lin_relu2_kernel(tc, xT, xr, w_words, w_scales, b, gate, offs, 
                 window_v[:].indirect(offsets_of(e * C, C)), squares[e][:], gates[:, e * C : (e + 1) * C], Alu.mult
             )
 
-        for e in (0, 2, 1, 3):
+        for e in ORDER:
             relu(e)
             square(e)
 
-        scatter_by_vector(0)
-        for e in (2, 1):
+        scatter_by_vector(ORDER[0])
+        for e in ORDER[1:3]:
             gated = keep.tile([P, C], F32, name=f"gated{e}")
             nc.vector.tensor_tensor(gated[:], squares[e][:], gates[:, e * C : (e + 1) * C], Alu.mult)
             nc.scalar.activation(window_s[:].indirect(offsets_of(e * C, C)), gated[:], Act.Copy)
-        scatter_by_vector(3)
+        scatter_by_vector(ORDER[3])
 
         nc.vector.tensor_tensor(partial[:], window_v[:], resid[:], Alu.add)
         t0 = 0

@@ -22,8 +22,10 @@ FP8X4 = mybir.dt.float8_e4m3fn_x4
 Act = mybir.ActivationFunctionType
 Alu = mybir.AluOpType
 
-BY_VECTOR = (512, 480, 416)
+BY_VECTOR = (576, 576, 416)
 ORDER = (0, 3, 1, 2)
+
+WIDTHS = (512, 384, 256, 128, 64)
 
 STORES = (256, 320, 320, 320, 320)
 
@@ -83,29 +85,42 @@ def tile_moe_res_lin_relu2_kernel(tc, xT, xr, w_words, w_scales, b, gate, offs, 
         def offsets_of(j0, slots):
             return offsets[:, j0 // OFFSETS_PER_COLUMN : (j0 + slots) // OFFSETS_PER_COLUMN]
 
-        def quantise(a, packed, j0, slots):
-            nc.vector.quantize_mx(
-                out=codes[a][:, j0 : j0 + slots].bitcast(FP8X4),
-                scales=scales[a][:, j0 : j0 + slots],
-                in_=packed[:, j0 : j0 + slots, :].rearrange("p t r -> p (t r)"),
-            )
+        def quantise(a, j0, packed):
+            i0 = 0
+            while i0 < packed.shape[1]:
+                slots = max(w for w in WIDTHS if w <= packed.shape[1] - i0)
+                nc.vector.quantize_mx(
+                    out=codes[a][:, j0 + i0 : j0 + i0 + slots].bitcast(FP8X4),
+                    scales=scales[a][:, j0 + i0 : j0 + i0 + slots],
+                    in_=packed[:, i0 : i0 + slots, :].rearrange("p t r -> p (t r)"),
+                )
+                i0 += slots
 
-        for a in range(PASSES):
+        for a in range(PASSES - 1):
             split = SLOTS - BY_VECTOR[a]
-            packed = keep.tile([P, SLOTS, PACK], BF16, name=f"packed{a}", align_bytes=64)
+            packed_s = keep.tile([P, split, PACK], BF16, name=f"packed_s{a}", tag=f"packed{a}", align_bytes=64)
+            planes = keep.tile([P, PACK, BY_VECTOR[a]], BF16, name=f"planes{a}")
             for r in range(PACK):
                 row = rows[a * PACK + r]
-                nc.vector.tensor_copy(out=packed[:, split:, r], in_=row[:].indirect(offsets_of(split, SLOTS - split)))
-                ends = (C, split) if a == PASSES - 1 and r == PACK - 1 else (split,)
-                j0 = 0
-                for j1 in ends:
-                    nc.scalar.activation(packed[:, j0:j1, r], row[:].indirect(offsets_of(j0, j1 - j0)), Act.Copy)
-                    j0 = j1
-            if a < PASSES - 1:
-                quantise(a, packed, 0, SLOTS)
-            else:
-                for e in ORDER:
-                    quantise(a, packed, e * C, C)
+                nc.vector.tensor_copy(out=planes[:, r, :], in_=row[:].indirect(offsets_of(split, SLOTS - split)))
+                nc.scalar.activation(packed_s[:, :, r], row[:].indirect(offsets_of(0, split)), Act.Copy)
+            quantise(a, 0, packed_s[:])
+            packed_v = keep.tile([P, BY_VECTOR[a], PACK], BF16, name=f"packed_v{a}", tag=f"packed{a}", align_bytes=64)
+            nc.gpsimd.tensor_copy(out=packed_v[:], in_=planes[:].rearrange("p r t -> p t r"))
+            quantise(a, split, packed_v[:])
+
+        a = PASSES - 1
+        split = SLOTS - BY_VECTOR[a]
+        packed = keep.tile([P, SLOTS, PACK], BF16, name="packed_last", align_bytes=64)
+        for r in range(PACK):
+            row = rows[a * PACK + r]
+            nc.vector.tensor_copy(out=packed[:, split:, r], in_=row[:].indirect(offsets_of(split, SLOTS - split)))
+            j0 = 0
+            for j1 in (C, split) if r == PACK - 1 else (split,):
+                nc.scalar.activation(packed[:, j0:j1, r], row[:].indirect(offsets_of(j0, j1 - j0)), Act.Copy)
+                j0 = j1
+        for e in ORDER:
+            quantise(a, e * C, packed[:, e * C : (e + 1) * C, :])
 
         accs = [psum.tile([P, C], F32, name=f"acc{e}") for e in range(E)]
         for a in range(PASSES):

@@ -22,10 +22,10 @@ FP8X4 = mybir.dt.float8_e4m3fn_x4
 Act = mybir.ActivationFunctionType
 Alu = mybir.AluOpType
 
-BY_VECTOR = (576, 576, 416)
-ORDER = (0, 3, 1, 2)
+BY_VECTOR = (448, 448, 416)
+ORDER = (3, 0, 2, 1)
 
-WIDTHS = (512, 384, 256, 128, 64)
+HELD_BY_ROW = 1
 
 STORES = (256, 320, 320, 320, 320)
 
@@ -46,7 +46,6 @@ def tile_moe_res_lin_relu2_kernel(tc, xT, xr, w_words, w_scales, b, gate, offs, 
         window_v = keep.tile([P, T], F32, name="window_v")
         partial = keep.tile([P, T], F32, name="partial")
         total = keep.tile([P, T], F32, name="total")
-        codes = [keep.tile([P, SLOTS], U32, name=f"codes{a}", align_bytes=64) for a in range(PASSES)]
         scales = [keep.tile([P, SLOTS], U8, name=f"scales{a}", align_bytes=64) for a in range(PASSES)]
 
         nc.vector.memset(w_bytes[:].rearrange("p g n -> p (g n)").bitcast(I32), 0)
@@ -63,7 +62,7 @@ def tile_moe_res_lin_relu2_kernel(tc, xT, xr, w_words, w_scales, b, gate, offs, 
         for a in range(PASSES):
             of_pass = xT[a * P * PACK : (a + 1) * P * PACK, :].rearrange("(p r) t -> p r t", r=PACK)
             for r in range(PACK):
-                row = keep.tile([P, T], F32, name=f"row{a}_{r}")
+                row = keep.tile([P, T], F32, name=f"row{a}_{r}", tag=f"row{a}_{r}", align_bytes=64)
                 nc.sync.dma_start(out=row[:], in_=of_pass[:, r, :])
                 rows.append(row)
                 if a == 0 and r == 0:
@@ -76,51 +75,53 @@ def tile_moe_res_lin_relu2_kernel(tc, xT, xr, w_words, w_scales, b, gate, offs, 
         load_weights(ORDER[0], 1)
         nc.sync.dma_start(out=bias[:], in_=b)
         load_weights(ORDER[1], 1)
-        nc.sync.dma_start(out=gates[:, :C], in_=gate[:, :C])
+        nc.sync.dma_start(out=gates[:, 3 * C :], in_=gate[:, 3 * C :])
         load_weights(ORDER[2], 1)
         load_weights(ORDER[3], 1)
-        nc.sync.dma_start(out=gates[:, C:], in_=gate[:, C:])
+        nc.sync.dma_start(out=gates[:, : 3 * C], in_=gate[:, : 3 * C])
         nc.sync.dma_start(out=resid[:], in_=xr)
 
         def offsets_of(j0, slots):
             return offsets[:, j0 // OFFSETS_PER_COLUMN : (j0 + slots) // OFFSETS_PER_COLUMN]
 
-        def quantise(a, j0, packed):
-            i0 = 0
-            while i0 < packed.shape[1]:
-                slots = max(w for w in WIDTHS if w <= packed.shape[1] - i0)
-                nc.vector.quantize_mx(
-                    out=codes[a][:, j0 + i0 : j0 + i0 + slots].bitcast(FP8X4),
-                    scales=scales[a][:, j0 + i0 : j0 + i0 + slots],
-                    in_=packed[:, i0 : i0 + slots, :].rearrange("p t r -> p (t r)"),
-                )
-                i0 += slots
+        def weave(copy, pairs, packed, j0, slots):
+            copy(
+                out=packed[:, j0 : j0 + slots, :].bitcast(U32),
+                in_=pairs[:, :, j0 : j0 + slots, :].bitcast(U32).rearrange("p h t o -> p t (h o)"),
+            )
 
-        for a in range(PASSES - 1):
+        def quantise(a, packed, j0, slots):
+            nc.vector.quantize_mx(
+                out=codes[a][:, j0 : j0 + slots].bitcast(FP8X4),
+                scales=scales[a][:, j0 : j0 + slots],
+                in_=packed[:, j0 : j0 + slots, :].rearrange("p t r -> p (t r)"),
+            )
+
+        codes = []
+        for a in range(PASSES):
+            last = a == PASSES - 1
+            tag = "codes_last" if last else f"row{a + 1}_{HELD_BY_ROW}"
             split = SLOTS - BY_VECTOR[a]
-            packed_s = keep.tile([P, split, PACK], BF16, name=f"packed_s{a}", tag=f"packed{a}", align_bytes=64)
-            planes = keep.tile([P, PACK, BY_VECTOR[a]], BF16, name=f"planes{a}")
+            pairs = keep.tile([P, 2, SLOTS, 2], BF16, name=f"pairs{a}")
+            packed = keep.tile([P, SLOTS, PACK], BF16, name=f"packed{a}", align_bytes=64)
             for r in range(PACK):
                 row = rows[a * PACK + r]
-                nc.vector.tensor_copy(out=planes[:, r, :], in_=row[:].indirect(offsets_of(split, SLOTS - split)))
-                nc.scalar.activation(packed_s[:, :, r], row[:].indirect(offsets_of(0, split)), Act.Copy)
-            quantise(a, 0, packed_s[:])
-            packed_v = keep.tile([P, BY_VECTOR[a], PACK], BF16, name=f"packed_v{a}", tag=f"packed{a}", align_bytes=64)
-            nc.gpsimd.tensor_copy(out=packed_v[:], in_=planes[:].rearrange("p r t -> p t r"))
-            quantise(a, split, packed_v[:])
-
-        a = PASSES - 1
-        split = SLOTS - BY_VECTOR[a]
-        packed = keep.tile([P, SLOTS, PACK], BF16, name="packed_last", align_bytes=64)
-        for r in range(PACK):
-            row = rows[a * PACK + r]
-            nc.vector.tensor_copy(out=packed[:, split:, r], in_=row[:].indirect(offsets_of(split, SLOTS - split)))
-            j0 = 0
-            for j1 in (C, split) if r == PACK - 1 else (split,):
-                nc.scalar.activation(packed[:, j0:j1, r], row[:].indirect(offsets_of(j0, j1 - j0)), Act.Copy)
-                j0 = j1
-        for e in ORDER:
-            quantise(a, e * C, packed[:, e * C : (e + 1) * C, :])
+                nc.vector.tensor_copy(
+                    out=pairs[:, r // 2, split:, r % 2], in_=row[:].indirect(offsets_of(split, SLOTS - split))
+                )
+                j0 = 0
+                for j1 in (C, split) if last and r == PACK - 1 else (split,):
+                    nc.scalar.activation(pairs[:, r // 2, j0:j1, r % 2], row[:].indirect(offsets_of(j0, j1 - j0)), Act.Copy)
+                    j0 = j1
+            codes.append(keep.tile([P, SLOTS], U32, name=f"codes{a}", tag=tag, align_bytes=64))
+            if not last:
+                weave(nc.gpsimd.tensor_copy, pairs, packed, 0, SLOTS)
+                quantise(a, packed, 0, SLOTS)
+                continue
+            copies = (nc.gpsimd.tensor_copy, nc.scalar.copy, nc.vector.tensor_copy, nc.vector.tensor_copy)
+            for e in ORDER:
+                weave(copies[e], pairs, packed, e * C, C)
+                quantise(a, packed, e * C, C)
 
         accs = [psum.tile([P, C], F32, name=f"acc{e}") for e in range(E)]
         for a in range(PASSES):

@@ -22,10 +22,8 @@ FP8X4 = mybir.dt.float8_e4m3fn_x4
 Act = mybir.ActivationFunctionType
 Alu = mybir.AluOpType
 
-BY_VECTOR = (448, 448, 416)
-ORDER = (3, 0, 2, 1)
-
-HELD_BY_ROW = 1
+BY_VECTOR = ((512, 512), (576, 384), (544, 256))
+ORDER = (3, 0, 1, 2)
 
 STORES = (256, 320, 320, 320, 320)
 
@@ -84,44 +82,48 @@ def tile_moe_res_lin_relu2_kernel(tc, xT, xr, w_words, w_scales, b, gate, offs, 
         def offsets_of(j0, slots):
             return offsets[:, j0 // OFFSETS_PER_COLUMN : (j0 + slots) // OFFSETS_PER_COLUMN]
 
-        def weave(copy, pairs, packed, j0, slots):
+        def weave(copy, pairs, packed, j0):
+            slots = packed.shape[1]
             copy(
-                out=packed[:, j0 : j0 + slots, :].bitcast(U32),
+                out=packed.bitcast(U32),
                 in_=pairs[:, :, j0 : j0 + slots, :].bitcast(U32).rearrange("p h t o -> p t (h o)"),
             )
 
-        def quantise(a, packed, j0, slots):
+        def quantise(a, packed, words, j0):
             nc.vector.quantize_mx(
-                out=codes[a][:, j0 : j0 + slots].bitcast(FP8X4),
-                scales=scales[a][:, j0 : j0 + slots],
-                in_=packed[:, j0 : j0 + slots, :].rearrange("p t r -> p (t r)"),
+                out=words.bitcast(FP8X4),
+                scales=scales[a][:, j0 : j0 + packed.shape[1]],
+                in_=packed.rearrange("p t r -> p (t r)"),
             )
 
-        codes = []
-        for a in range(PASSES):
-            last = a == PASSES - 1
-            tag = "codes_last" if last else f"row{a + 1}_{HELD_BY_ROW}"
-            split = SLOTS - BY_VECTOR[a]
+        def gather(a):
             pairs = keep.tile([P, 2, SLOTS, 2], BF16, name=f"pairs{a}")
-            packed = keep.tile([P, SLOTS, PACK], BF16, name=f"packed{a}", align_bytes=64)
             for r in range(PACK):
+                split = SLOTS - BY_VECTOR[a][r // 2]
                 row = rows[a * PACK + r]
                 nc.vector.tensor_copy(
                     out=pairs[:, r // 2, split:, r % 2], in_=row[:].indirect(offsets_of(split, SLOTS - split))
                 )
-                j0 = 0
-                for j1 in (C, split) if last and r == PACK - 1 else (split,):
+                for j0, j1 in ((0, C), (C, split)) if a * PACK + r == len(rows) - 1 else ((0, split),):
                     nc.scalar.activation(pairs[:, r // 2, j0:j1, r % 2], row[:].indirect(offsets_of(j0, j1 - j0)), Act.Copy)
-                    j0 = j1
-            codes.append(keep.tile([P, SLOTS], U32, name=f"codes{a}", tag=tag, align_bytes=64))
-            if not last:
-                weave(nc.gpsimd.tensor_copy, pairs, packed, 0, SLOTS)
-                quantise(a, packed, 0, SLOTS)
-                continue
-            copies = (nc.gpsimd.tensor_copy, nc.scalar.copy, nc.vector.tensor_copy, nc.vector.tensor_copy)
-            for e in ORDER:
-                weave(copies[e], pairs, packed, e * C, C)
-                quantise(a, packed, e * C, C)
+            return pairs
+
+        codes = []
+        for a in range(PASSES - 1):
+            pairs = gather(a)
+            packed = keep.tile([P, SLOTS, PACK], BF16, name=f"packed{a}", align_bytes=64)
+            codes.append(keep.tile([P, SLOTS], U32, name=f"codes{a}", tag=f"row{a + 1}_1", align_bytes=64))
+            weave(nc.gpsimd.tensor_copy, pairs, packed[:], 0)
+            quantise(a, packed[:], codes[a][:], 0)
+
+        pairs = gather(PASSES - 1)
+        packed = keep.tile([P, SLOTS, PACK], BF16, name="packed_last", align_bytes=64)
+        codes.append(keep.tile([P, SLOTS], U32, name="codes_last", align_bytes=64))
+        for pair in (ORDER[:2], ORDER[:1:-1]):
+            for e in pair:
+                weave(nc.scalar.copy if e == 1 else nc.vector.tensor_copy, pairs, packed[:, e * C : (e + 1) * C, :], e * C)
+            for e in pair if pair == ORDER[:2] else pair[::-1]:
+                quantise(PASSES - 1, packed[:, e * C : (e + 1) * C, :], codes[-1][:, e * C : (e + 1) * C], e * C)
 
         accs = [psum.tile([P, C], F32, name=f"acc{e}") for e in range(E)]
         for a in range(PASSES):

@@ -73,9 +73,9 @@ def tile_moe_res_lin_relu2_kernel(tc, xT, xr, w_words, w_scales, b, gate, offs, 
         load_weights(ORDER[0], 1)
         nc.sync.dma_start(out=bias[:], in_=b)
         load_weights(ORDER[1], 1)
-        nc.sync.dma_start(out=gates[:, 3 * C :], in_=gate[:, 3 * C :])
         load_weights(ORDER[2], 1)
         load_weights(ORDER[3], 1)
+        nc.sync.dma_start(out=gates[:, 3 * C :], in_=gate[:, 3 * C :])
         nc.sync.dma_start(out=gates[:, : 3 * C], in_=gate[:, : 3 * C])
         nc.sync.dma_start(out=resid[:], in_=xr)
 

@@ -23,7 +23,7 @@ Act = mybir.ActivationFunctionType
 Alu = mybir.AluOpType
 
 BY_VECTOR = ((512, 512), (576, 384), (544, 256))
-ORDER = (3, 0, 1, 2)
+ORDER = (0, 1, 2, 3)
 
 STORES = (256, 320, 320, 320, 320)
 
@@ -75,18 +75,18 @@ def tile_moe_res_lin_relu2_kernel(tc, xT, xr, w_words, w_scales, b, gate, offs, 
         load_weights(ORDER[1], 1)
         load_weights(ORDER[2], 1)
         load_weights(ORDER[3], 1)
-        nc.sync.dma_start(out=gates[:, 3 * C :], in_=gate[:, 3 * C :])
-        nc.sync.dma_start(out=gates[:, : 3 * C], in_=gate[:, : 3 * C])
+        nc.sync.dma_start(out=gates[:, :C], in_=gate[:, :C])
+        nc.sync.dma_start(out=gates[:, C:], in_=gate[:, C:])
         nc.sync.dma_start(out=resid[:], in_=xr)
 
         def offsets_of(j0, slots):
             return offsets[:, j0 // OFFSETS_PER_COLUMN : (j0 + slots) // OFFSETS_PER_COLUMN]
 
-        def weave(copy, pairs, packed, j0):
+        def weave(copy, pairs, packed, j0, run):
             slots = packed.shape[1]
             copy(
-                out=packed.bitcast(U32),
-                in_=pairs[:, :, j0 : j0 + slots, :].bitcast(U32).rearrange("p h t o -> p t (h o)"),
+                out=packed.bitcast(U32).rearrange("p (c i) h -> p c h i", i=run),
+                in_=pairs[:, :, j0 : j0 + slots, :].bitcast(U32).rearrange("p h (c i) o -> p c h (i o)", i=run),
             )
 
         def quantise(a, packed, words, j0):
@@ -99,12 +99,12 @@ def tile_moe_res_lin_relu2_kernel(tc, xT, xr, w_words, w_scales, b, gate, offs, 
         def gather(a):
             pairs = keep.tile([P, 2, SLOTS, 2], BF16, name=f"pairs{a}")
             for r in range(PACK):
-                split = SLOTS - BY_VECTOR[a][r // 2]
+                split = BY_VECTOR[a][r // 2]
                 row = rows[a * PACK + r]
                 nc.vector.tensor_copy(
-                    out=pairs[:, r // 2, split:, r % 2], in_=row[:].indirect(offsets_of(split, SLOTS - split))
+                    out=pairs[:, r // 2, :split, r % 2], in_=row[:].indirect(offsets_of(0, split))
                 )
-                for j0, j1 in ((0, C), (C, split)) if a * PACK + r == len(rows) - 1 else ((0, split),):
+                for j0, j1 in ((split, 2 * C), (2 * C, SLOTS)) if a * PACK + r == len(rows) - 1 else ((split, SLOTS),):
                     nc.scalar.activation(pairs[:, r // 2, j0:j1, r % 2], row[:].indirect(offsets_of(j0, j1 - j0)), Act.Copy)
             return pairs
 
@@ -113,7 +113,7 @@ def tile_moe_res_lin_relu2_kernel(tc, xT, xr, w_words, w_scales, b, gate, offs, 
             pairs = gather(a)
             packed = keep.tile([P, SLOTS, PACK], BF16, name=f"packed{a}", align_bytes=64)
             codes.append(keep.tile([P, SLOTS], U32, name=f"codes{a}", tag=f"row{a + 1}_1", align_bytes=64))
-            weave(nc.gpsimd.tensor_copy, pairs, packed[:], 0)
+            weave(nc.gpsimd.tensor_copy, pairs, packed[:], 0, 1)
             quantise(a, packed[:], codes[a][:], 0)
 
         pairs = gather(PASSES - 1)
@@ -121,7 +121,7 @@ def tile_moe_res_lin_relu2_kernel(tc, xT, xr, w_words, w_scales, b, gate, offs, 
         codes.append(keep.tile([P, SLOTS], U32, name="codes_last", align_bytes=64))
         for pair in (ORDER[:2], ORDER[:1:-1]):
             for e in pair:
-                weave(nc.scalar.copy if e == 1 else nc.vector.tensor_copy, pairs, packed[:, e * C : (e + 1) * C, :], e * C)
+                weave(nc.scalar.copy if e == 2 else nc.vector.tensor_copy, pairs, packed[:, e * C : (e + 1) * C, :], e * C, 2)
             for e in pair if pair == ORDER[:2] else pair[::-1]:
                 quantise(PASSES - 1, packed[:, e * C : (e + 1) * C, :], codes[-1][:, e * C : (e + 1) * C], e * C)
 

from contextlib import ExitStack

import concourse.mybir as mybir

K, T, E, C, N = 1536, 1536, 4, 256, 128
SLOTS = E * C
P = 128
PACK = 4
PASSES = K // (P * PACK)
SCALE_ROWS = 4
OFFSETS_PER_COLUMN = 16

FLOPS = 2 * K * N * SLOTS

F32 = mybir.dt.float32
BF16 = mybir.dt.bfloat16
I32 = mybir.dt.int32
U32 = mybir.dt.uint32
U16 = mybir.dt.uint16
U8 = mybir.dt.uint8
FP8X4 = mybir.dt.float8_e4m3fn_x4
Act = mybir.ActivationFunctionType
Alu = mybir.AluOpType

BY_VECTOR = ((512, 512), (576, 384), (544, 256))
ORDER = (0, 1, 2, 3)

STORES = (256, 320, 320, 320, 320)


def tile_moe_res_lin_relu2_kernel(tc, xT, xr, w_words, w_scales, b, gate, offs, out):
    nc = tc.nc
    with ExitStack() as ctx:
        keep = ctx.enter_context(tc.tile_pool(name="keep", bufs=1))
        psum = ctx.enter_context(tc.psum_pool(name="psum", bufs=1))

        offsets = keep.tile([P, SLOTS // OFFSETS_PER_COLUMN], U16, name="offsets")
        w_codes = keep.tile([P, E * PASSES, N], U32, name="w_codes", align_bytes=64)
        w_bytes = keep.tile([P, E * PASSES, N], U8, name="w_bytes", align_bytes=64)
        bias = keep.tile([P, E], F32, name="bias")
        gates = keep.tile([P, SLOTS], F32, name="gates")
        resid = keep.tile([P, T], F32, name="resid")
        window_s = keep.tile([P, T], F32, name="window_s")
        window_v = keep.tile([P, T], F32, name="window_v")
        partial = keep.tile([P, T], F32, name="partial")
        total = keep.tile([P, T], F32, name="total")
        scales = [keep.tile([P, SLOTS], U8, name=f"scales{a}", align_bytes=64) for a in range(PASSES)]

        nc.vector.memset(w_bytes[:].rearrange("p g n -> p (g n)").bitcast(I32), 0)
        nc.vector.memset(window_v[:], 0.0)
        nc.scalar.activation(window_s[:], window_v[:], Act.Copy)

        def load_weights(e, experts):
            nc.sync.dma_start(
                out=w_codes[:, e * PASSES : (e + experts) * PASSES, :].rearrange("p g n -> p (g n)").bitcast(I32),
                in_=w_words[e : e + experts].rearrange("e a p n r -> p (e a) (n r)").bitcast(I32),
            )

        rows = []
        for a in range(PASSES):
            of_pass = xT[a * P * PACK : (a + 1) * P * PACK, :].rearrange("(p r) t -> p r t", r=PACK)
            for r in range(PACK):
                row = keep.tile([P, T], F32, name=f"row{a}_{r}", tag=f"row{a}_{r}", align_bytes=64)
                nc.sync.dma_start(out=row[:], in_=of_pass[:, r, :])
                rows.append(row)
                if a == 0 and r == 0:
                    nc.sync.dma_start(offsets[:], offs)
        for q in range(SCALE_ROWS):
            nc.sync.dma_start(
                out=w_bytes[q:P:32, :, :].bitcast(I32),
                in_=w_scales[:, :, q:16:SCALE_ROWS, :].rearrange("e a q n -> q (e a) n").bitcast(I32),
            )
        load_weights(ORDER[0], 1)
        nc.sync.dma_start(out=bias[:], in_=b)
        load_weights(ORDER[1], 1)
        load_weights(ORDER[2], 1)
        load_weights(ORDER[3], 1)
        nc.sync.dma_start(out=gates[:, :C], in_=gate[:, :C])
        nc.sync.dma_start(out=gates[:, C:], in_=gate[:, C:])
        nc.sync.dma_start(out=resid[:], in_=xr)

        def offsets_of(j0, slots):
            return offsets[:, j0 // OFFSETS_PER_COLUMN : (j0 + slots) // OFFSETS_PER_COLUMN]

        def weave(copy, pairs, packed, j0, run):
            slots = packed.shape[1]
            copy(
                out=packed.bitcast(U32).rearrange("p (c i) h -> p c h i", i=run),
                in_=pairs[:, :, j0 : j0 + slots, :].bitcast(U32).rearrange("p h (c i) o -> p c h (i o)", i=run),
            )

        def quantise(a, packed, words, j0):
            nc.vector.quantize_mx(
                out=words.bitcast(FP8X4),
                scales=scales[a][:, j0 : j0 + packed.shape[1]],
                in_=packed.rearrange("p t r -> p (t r)"),
            )

        def gather(a):
            pairs = keep.tile([P, 2, SLOTS, 2], BF16, name=f"pairs{a}")
            for r in range(PACK):
                split = BY_VECTOR[a][r // 2]
                row = rows[a * PACK + r]
                nc.vector.tensor_copy(
                    out=pairs[:, r // 2, :split, r % 2], in_=row[:].indirect(offsets_of(0, split))
                )
                for j0, j1 in ((split, 2 * C), (2 * C, SLOTS)) if a * PACK + r == len(rows) - 1 else ((split, SLOTS),):
                    nc.scalar.activation(pairs[:, r // 2, j0:j1, r % 2], row[:].indirect(offsets_of(j0, j1 - j0)), Act.Copy)
            return pairs

        codes = []
        for a in range(PASSES - 1):
            pairs = gather(a)
            packed = keep.tile([P, SLOTS, PACK], BF16, name=f"packed{a}", align_bytes=64)
            codes.append(keep.tile([P, SLOTS], U32, name=f"codes{a}", tag=f"row{a + 1}_1", align_bytes=64))
            weave(nc.gpsimd.tensor_copy, pairs, packed[:], 0, 1)
            quantise(a, packed[:], codes[a][:], 0)

        pairs = gather(PASSES - 1)
        packed = keep.tile([P, SLOTS, PACK], BF16, name="packed_last", align_bytes=64)
        codes.append(keep.tile([P, SLOTS], U32, name="codes_last", align_bytes=64))
        for pair in (ORDER[:2], ORDER[:1:-1]):
            for e in pair:
                weave(nc.scalar.copy if e == 2 else nc.vector.tensor_copy, pairs, packed[:, e * C : (e + 1) * C, :], e * C, 2)
            for e in pair if pair == ORDER[:2] else pair[::-1]:
                quantise(PASSES - 1, packed[:, e * C : (e + 1) * C, :], codes[-1][:, e * C : (e + 1) * C], e * C)

        accs = [psum.tile([P, C], F32, name=f"acc{e}") for e in range(E)]
        for a in range(PASSES):
            for e in ORDER:
                cols = slice(e * C, (e + 1) * C)
                nc.tensor.matmul_mx(
                    out=accs[e][:],
                    lhsT=w_codes[:, e * PASSES + a, :].bitcast(FP8X4),
                    lhsT_scale=w_bytes[:, e * PASSES + a, :],
                    rhs=codes[a][:, cols].bitcast(FP8X4),
                    rhs_scale=scales[a][:, cols],
                    start=(a == 0),
                    stop=(a == PASSES - 1),
                )

        relus = [keep.tile([P, C], F32, name=f"relu{e}") for e in range(E)]
        squares = [keep.tile([P, C], F32, name=f"square{e}") for e in range(E)]

        def relu(e):
            nc.scalar.activation(relus[e][:], accs[e][:], Act.Relu, bias=bias[:, e : e + 1])

        def square(e):
            nc.scalar.activation(squares[e][:], relus[e][:], Act.Square)

        def scatter_by_vector(e):
            nc.vector.tensor_tensor(
                window_v[:].indirect(offsets_of(e * C, C)), squares[e][:], gates[:, e * C : (e + 1) * C], Alu.mult
            )

        for e in ORDER:
            relu(e)
            square(e)

        scatter_by_vector(ORDER[0])
        for e in ORDER[1:3]:
            gated = keep.tile([P, C], F32, name=f"gated{e}")
            nc.vector.tensor_tensor(gated[:], squares[e][:], gates[:, e * C : (e + 1) * C], Alu.mult)
            nc.scalar.activation(window_s[:].indirect(offsets_of(e * C, C)), gated[:], Act.Copy)
        scatter_by_vector(ORDER[3])

        nc.vector.tensor_tensor(partial[:], window_v[:], resid[:], Alu.add)
        t0 = 0
        for width in STORES:
            cols = slice(t0, t0 + width)
            nc.vector.tensor_tensor(total[:, cols], window_s[:, cols], partial[:, cols], Alu.add)
            nc.sync.dma_start(out=out[:, cols], in_=total[:, cols])
            t0 += width
